import numpy as np
import ml_dtypes


def mxq(x, axis, fmt="e4m3"):
    dtype, down = {"e4m3": (ml_dtypes.float8_e4m3fn, 7), "e5m2": (ml_dtypes.float8_e5m2, 14)}[fmt]
    v = np.moveaxis(np.asarray(x, np.float32).astype(ml_dtypes.bfloat16).astype(np.float64), axis, -1)
    blocks = v.reshape(v.shape[:-1] + (-1, 32))
    amax = np.abs(blocks).max(-1, keepdims=True)
    byte = np.maximum(np.where(amax > 0, np.frexp(amax)[1] - 1 + 127, 0) - down, 1)
    scale = np.exp2(byte - 127.0)
    codes = (blocks / scale).astype(np.float32).astype(dtype).astype(np.float64)
    return np.moveaxis((codes * scale).reshape(v.shape), -1, axis)


WIDE = False


def mx_kscale(k):
    if not WIDE:
        return np.ones(k)
    levels = np.array([10, -10, 5, -5, 0])
    if k % 512:
        return np.exp2(np.random.permutation(np.resize(levels, k // 32))).repeat(32)
    a = np.empty((k // 512, 16))
    for p in range(k // 512):
        a[p, :8] = np.random.permutation(np.resize(levels, 8))
        for g in range(8):
            far = levels[np.abs(levels - a[p, g]) >= 10]
            a[p, g + 8] = far[np.random.randint(len(far))]
    return np.exp2(a.ravel()).repeat(32)


def f64(x):
    return np.asarray(x).astype(np.float64)


def striped(idx):
    return np.tile(np.asarray(idx).reshape(-1, 16).T, (8, 1)).astype(np.uint16)


def unstriped(offs):
    return offs[:16].T.reshape(-1).astype(np.int64)


E2M1 = np.array([0.0, 0.5, 1.0, 1.5, 2.0, 3.0, 4.0, 6.0, -0.0, -0.5, -1.0, -1.5, -2.0, -3.0, -4.0, -6.0])


def pack_weight(w, fmt):
    k, n = w.shape
    w = f64(np.asarray(w, np.float32).astype(ml_dtypes.bfloat16)).reshape(k // 32, 32, n)
    amax = np.abs(w).max(1)
    if fmt == "e4m3":
        byte = np.frexp(amax)[1] - 1 + 127 - 7
    else:
        mant, ex = np.frexp(amax / 6.0)
        byte = np.where(mant > 0.5, ex, ex - 1) + 127
    byte = np.clip(np.where(amax > 0, byte, 1), 1, 254)
    scaled = (w * np.exp2(127.0 - byte)[:, None, :]).reshape(k, n).astype(np.float32)
    by_word = np.ascontiguousarray(scaled.reshape(k // 512, 128, 4, n).transpose(0, 1, 3, 2))
    if fmt == "e4m3":
        words = by_word.astype(ml_dtypes.float8_e4m3fn).view(np.uint8)
    else:
        c = by_word.astype(ml_dtypes.float4_e2m1fn).view(np.uint8) & 0xF
        words = (c[..., 0::2] | (c[..., 1::2] << 4)).reshape(k // 512, 128, 2 * n)
    return np.ascontiguousarray(words), np.ascontiguousarray(byte.astype(np.uint8).reshape(k // 512, 16, n))


def unpack_weight(words, scales, fmt):
    g, _, n = scales.shape
    words = np.ascontiguousarray(words).reshape(g, 128, n, -1)
    if fmt == "e4m3":
        vals = words.view(ml_dtypes.float8_e4m3fn).astype(np.float64)
    else:
        nib = np.empty((g, 128, n, 4), np.uint8)
        nib[..., 0::2] = words & 0xF
        nib[..., 1::2] = words >> 4
        vals = E2M1[nib]
    vals = vals * np.repeat(np.exp2(scales.astype(np.float64) - 127.0), 8, axis=1)[..., None]
    return vals.transpose(0, 1, 3, 2).reshape(g * 512, n)


B, N, T, D, DV, NQ = 1, 1536, 4096, 512, 128, 128
PAGE = 512
CAP = 2.0


def setup_inputs():
    n = np.random.standard_normal
    pages = np.random.permutation(T // PAGE)[:B * N // PAGE]
    idx = (pages[:, None] * PAGE + np.arange(PAGE)[None, :]).reshape(-1)
    s = mx_kscale(D)[:, None]
    u = np.ones(T)
    u[idx] = mx_kscale(B * N)
    r = np.random.uniform(0.5, 2.0, T)
    qp = [pack_weight(x, "e4m3") for x in n((B, D, NQ)) * s * (0.80 / np.sqrt(D))]
    k = n((D, T)) / s
    v = n((DV, T)) / (u * r)
    kp = pack_weight(k, "e4m3")
    vp = pack_weight(v.T, "e4m3")
    return {
        "q_words": np.stack([x[0] for x in qp]),
        "q_scales": np.stack([x[1] for x in qp]),
        "k_words": kp[0],
        "k_scales": kp[1],
        "v_words": vp[0],
        "v_scales": vp[1],
        "vs": np.tile(u * r, (128, 1)).astype(np.float32),
        "kb": np.tile(n(T), (128, 1)).astype(np.float32),
        "offs": striped(idx),
        "voffs": striped((pages[:, None] * DV + np.arange(DV)[None, :]).reshape(-1)),
    }


def reference(q_words, q_scales, k_words, k_scales, v_words, v_scales, vs, kb, offs, voffs):
    idx = unstriped(offs)
    k = unpack_weight(k_words, k_scales, "e4m3")
    v = unpack_weight(v_words, v_scales, "e4m3")
    v = v.reshape(T // 512, 512, DV)[unstriped(voffs)[::DV] // DV].reshape(B, N, DV)
    pick = lambda x: x[:, idx].reshape(x.shape[0], B, N).transpose(1, 0, 2)
    q = np.stack([unpack_weight(q_words[b], q_scales[b], "e4m3") for b in range(B)])
    score = q.transpose(0, 2, 1) @ pick(k)
    score = score + pick(f64(kb))[:, :1, :]
    score = CAP * np.tanh(score / CAP)
    p = np.square(np.maximum(score, 0.0))
    total = p.sum(-1, keepdims=True) + 1.0
    w = p * pick(f64(vs))[:, :1, :]
    y = mxq(w, 2, "e4m3") @ v
    y = y / total
    return y

@@ -1,0 +1,196 @@
+from contextlib import ExitStack
+
+import concourse.mybir as mybir
+from concourse.masks import make_identity
+
+N, T, D, DV, NQ = 1536, 4096, 512, 128, 128
+PAGE = 512
+PAGES = N // PAGE
+POOL_PAGES = T // PAGE
+CAP = 2.0
+P = 128
+PACK = 4
+QUADRANTS = 4
+LIST_ROWS = 16
+DATA_ROW = 127
+
+FLOPS = 2 * NQ * N * D + 2 * NQ * N * DV
+BYTES = T * D + T * D // 32 + T * DV + T * DV // 32 + NQ * D + NQ * D // 32 + 2 * 4 * T + 2 * P * (N + PAGES * DV) // LIST_ROWS + 4 * NQ * DV
+
+F32 = mybir.dt.float32
+BF16 = mybir.dt.bfloat16
+I32 = mybir.dt.int32
+U32 = mybir.dt.uint32
+U16 = mybir.dt.uint16
+U8 = mybir.dt.uint8
+FP8X4 = mybir.dt.float8_e4m3fn_x4
+ALU = mybir.AluOpType
+ACT = mybir.ActivationFunctionType
+
+
+def tile_attend_pkv8q_rel2_cap_kb_kernel(
+    tc, q_words, q_scales, k_words, k_scales, v_words, v_scales, vs, kb, offs, voffs, out
+):
+    nc = tc.nc
+    with ExitStack() as ctx:
+        lists = ctx.enter_context(tc.tile_pool(name="lists", bufs=1))
+        held = ctx.enter_context(tc.tile_pool(name="held", bufs=1))
+        psum = ctx.enter_context(tc.psum_pool(name="psum", bufs=1))
+
+        key_list = lists.tile([P, N // LIST_ROWS], U16, name="key_list")
+        value_list = lists.tile([P, PAGES * DV // LIST_ROWS], U16, name="value_list")
+
+        def sb(shape, dtype, name, tag=None):
+            return held.tile(shape, dtype, name=name, tag=tag or name, align_bytes=64)
+
+        def bank(name, tag):
+            return psum.tile([P, PACK, P], F32, name=name, tag=tag)
+
+        kw_pool = sb([P, T], I32, "kw_pool", "d")
+        ks_pool = sb([P, T], U8, "ks_pool", "c")
+        vsc_pool = sb([P, POOL_PAGES * DV], U8, "vsc_pool", "e")
+        kb_pool = sb([P, T], F32, "kb_pool")
+        qw = sb([P, NQ], I32, "qw")
+        qs = sb([P, NQ], U8, "qs")
+        ident = sb([P, P], F32, "ident")
+        warm = sb([P, 1], F32, "warm")
+
+        nc.vector.memset(ks_pool[:].bitcast(I32), 0)
+        nc.vector.memset(qs[:].bitcast(I32), 0)
+        nc.vector.memset(vsc_pool[:].bitcast(I32), 0)
+        nc.vector.memset(kb_pool[0:DATA_ROW, :], 0.0)
+        make_identity(nc, ident[:])
+
+        nc.sync.dma_start(key_list[:], offs)
+        nc.sync.dma_start(value_list[:], voffs)
+        nc.sync.dma_start(qw[:], q_words[0, 0].rearrange("p q r -> p (q r)").bitcast(I32))
+        nc.sync.dma_start(kw_pool[:], k_words[0].rearrange("p t r -> p (t r)").bitcast(I32))
+        nc.scalar.dma_start(kb_pool[DATA_ROW : DATA_ROW + 1, :], kb[0:1, :])
+        for g in range(QUADRANTS):
+            nc.scalar.dma_start(ks_pool[32 * g : 32 * g + 4, :].bitcast(I32), k_scales[0, 4 * g : 4 * g + 4, :].bitcast(I32))
+        nc.scalar.activation(warm[:], ident[:, 0:1], ACT.Tanh)
+        for g in range(QUADRANTS):
+            nc.scalar.dma_start(qs[32 * g : 32 * g + 4, :].bitcast(I32), q_scales[0, 0, 4 * g : 4 * g + 4, :].bitcast(I32))
+        for g in range(QUADRANTS):
+            nc.sync.dma_start(
+                vsc_pool[32 * g : 32 * g + 4, :].bitcast(I32).rearrange("p (u e) -> p u e", u=POOL_PAGES),
+                v_scales[:, 4 * g : 4 * g + 4, :].rearrange("u f e -> f u e").bitcast(I32),
+            )
+
+        def page_list(e):
+            cols = PAGE // LIST_ROWS
+            return key_list[:, e * cols : (e + 1) * cols]
+
+        def page(e):
+            return slice(e * PAGE, (e + 1) * PAGE)
+
+        def turn(dst, row):
+            for t in range(PACK):
+                nc.tensor.transpose(dst[:, t, :], row[:, t:PAGE:PACK], ident[:])
+
+        kb_col = []
+        for e in range(PAGES):
+            row = sb([P, PAGE], F32, "kb_row%d" % e, "abf"[e])
+            nc.vector.tensor_copy(row[:], kb_pool[:].indirect(page_list(e)))
+            turned = bank("kb_t%d" % e, "p%d" % e)
+            turn(turned, row)
+            col = sb([P, PACK], F32, "kb_col%d" % e)
+            nc.scalar.copy(col[:], turned[:, :, DATA_ROW])
+            kb_col.append(col)
+
+        vw_pool = sb([P, POOL_PAGES * DV], I32, "vw_pool", "a")
+        nc.sync.dma_start(
+            vw_pool[:].rearrange("p (u e) -> p u e", u=POOL_PAGES),
+            v_words.rearrange("u p e r -> p u (e r)").bitcast(I32),
+        )
+        vs_pool = sb([P, T], F32, "vs_pool", "b")
+        nc.sync.dma_start(vs_pool[:], vs)
+
+        ks = sb([P, N], U8, "ks")
+        for e in range(PAGES):
+            nc.vector.tensor_copy(ks[:, page(e)], ks_pool[:].indirect(page_list(e)))
+        kw = sb([P, N], U32, "kw", "c")
+        for e in range(PAGES):
+            nc.vector.tensor_copy(kw[:, page(e)], kw_pool[:].bitcast(U32).indirect(page_list(e)))
+
+        def score(e, tag, tag_t):
+            scores = bank("scores%d" % e, tag)
+            flat = scores[:].rearrange("q t s -> q (t s)")
+            nc.tensor.matmul_mx(
+                flat, lhsT=qw[:].bitcast(FP8X4), lhsT_scale=qs[:], rhs=kw[:, page(e)].bitcast(FP8X4),
+                rhs_scale=ks[:, page(e)], start=True, stop=True,
+            )
+            dealt = sb([P, PACK, P], F32, "dealt%d" % e)
+            nc.scalar.copy(dealt[:], flat.rearrange("q (s t) -> q t s", t=PACK))
+            scores_t = bank("scores_t%d" % e, tag_t)
+            for t in range(PACK):
+                nc.tensor.transpose(scores_t[:, t, :], dealt[:, t, :], ident[:])
+            return scores_t
+
+        def positive(e, scores_t):
+            pos = sb([P, PACK, NQ], F32, "pos%d" % e)
+            for t in range(PACK):
+                nc.scalar.activation(pos[:, t, :], scores_t[:, t, :], ACT.Relu, bias=kb_col[e][:, t : t + 1])
+            return pos
+
+        def weigh(e, pos):
+            capped = sb([P, PACK, NQ], F32, "capped%d" % e)
+            nc.scalar.activation(capped[:], pos[:], ACT.Tanh, scale=1.0 / CAP)
+            p = sb([P, PACK, NQ], F32, "p%d" % e)
+            nc.scalar.activation(p[:], capped[:], ACT.Square, scale=CAP)
+            return p
+
+        st0 = score(0, "p0", "p2")
+        st1 = score(1, "p1", "p0")
+        pos0 = positive(0, st0)
+        st2 = score(2, "p2", "p1")
+        p_t = [weigh(0, pos0)]
+        p_t.append(weigh(1, positive(1, st1)))
+        p_t.append(weigh(2, positive(2, st2)))
+
+        vw = sb([P, PAGES * DV], U32, "vw", "d")
+        nc.vector.tensor_copy(vw[:], vw_pool[:].bitcast(U32).indirect(value_list[:]))
+        vsc = sb([P, PAGES * DV], U8, "vsc", "a")
+        nc.vector.tensor_copy(vsc[:], vsc_pool[:].indirect(value_list[:]))
+        vs_row = sb([P, N], F32, "vs_row", "e")
+        vs_t = []
+        for e in range(PAGES):
+            nc.vector.tensor_copy(vs_row[:, page(e)], vs_pool[:].indirect(page_list(e)))
+            turned = bank("vs_t%d" % e, ("p2", "p0", "p1")[e])
+            turn(turned, vs_row[:, page(e)])
+            vs_t.append(turned)
+
+        total = psum.tile([P, P], F32, name="total")
+        acc = psum.tile([P, DV], F32, name="acc")
+        for e in range(PAGES):
+            p = p_t[e]
+            for t in range(PACK):
+                nc.tensor.matmul(
+                    total[:], lhsT=p[:, t, :], rhs=ident[:], is_transpose=True,
+                    start=(e == 0 and t == 0), stop=(e == PAGES - 1 and t == PACK - 1),
+                )
+            w = sb([P, NQ * PACK], BF16, "w%d" % e)
+            nc.vector.tensor_tensor(
+                w[:].rearrange("s (c i t) -> s c t i", i=4, t=PACK),
+                p[:].rearrange("s t (c i) -> s c t i", i=4),
+                vs_t[e][:].rearrange("s t (c i) -> s c t i", i=4),
+                ALU.mult,
+            )
+            w_codes = sb([P, NQ], U32, "w_codes%d" % e)
+            w_scales = sb([P, NQ], U8, "w_scales%d" % e)
+            nc.vector.quantize_mx(w_codes[:].bitcast(FP8X4), w_scales[:], w[:])
+            cols = slice(e * DV, (e + 1) * DV)
+            nc.tensor.matmul_mx(
+                acc[:], lhsT=w_codes[:].bitcast(FP8X4), lhsT_scale=w_scales[:],
+                rhs=vw[:, cols].bitcast(FP8X4), rhs_scale=vsc[:, cols],
+                start=(e == 0), stop=(e == PAGES - 1),
+            )
+
+        parts = sb([P, P], F32, "parts")
+        denom = sb([P, 1], F32, "denom")
+        nc.vector.tensor_scalar(parts[:], total[:], 1.0, 1.0, op0=ALU.mult, op1=ALU.add, accum_out=denom[:])
+        inv = sb([P, 1], F32, "inv")
+        nc.vector.reciprocal(inv[:], denom[:])
+        y = sb([P, DV], F32, "y")
+        nc.scalar.activation(y[:], acc[:], ACT.Copy, scale=inv[:])
+        nc.sync.dma_start(out[0], y[:])

@@ -47,35 +47,35 @@ def tile_attend_pkv8q_rel2_cap_kb_kernel(
             return psum.tile([P, PACK, P], F32, name=name, tag=tag)
 
         kw_pool = sb([P, T], I32, "kw_pool", "d")
-        ks_pool = sb([P, T], U8, "ks_pool", "c")
-        vsc_pool = sb([P, POOL_PAGES * DV], U8, "vsc_pool", "e")
-        kb_pool = sb([P, T], F32, "kb_pool")
+        ks_pool = sb([P, T], U8, "ks_pool")
+        vsc_pool = sb([P, POOL_PAGES * DV], U8, "vsc_pool")
+        kb_pool = sb([P, T], F32, "kb_pool", "a")
         qw = sb([P, NQ], I32, "qw")
         qs = sb([P, NQ], U8, "qs")
         ident = sb([P, P], F32, "ident")
-        warm = sb([P, 1], F32, "warm")
+        warm = sb([P, 2], F32, "warm")
 
-        nc.vector.memset(ks_pool[:].bitcast(I32), 0)
-        nc.vector.memset(qs[:].bitcast(I32), 0)
-        nc.vector.memset(vsc_pool[:].bitcast(I32), 0)
-        nc.vector.memset(kb_pool[0:DATA_ROW, :], 0.0)
+        ks_words = ks_pool[:].bitcast(I32)
+        nc.gpsimd.memset(warm[:, 0:1], 0.0)
+        nc.vector.memset(ks_words[:, 0:511], 0)
+        nc.vector.memset(ks_words[:, 511:1024], 0)
+        nc.vector.memset(kb_pool[0:DATA_ROW, 0:615], 0.0)
+        nc.vector.memset(kb_pool[0:DATA_ROW, 615:1232], 0.0)
+        nc.gpsimd.memset(kb_pool[0:DATA_ROW, 1232:T], 0.0)
+        nc.gpsimd.memset(qs[:].bitcast(I32), 0)
         make_identity(nc, ident[:])
+        nc.gpsimd.memset(vsc_pool[:].bitcast(I32), 0)
 
         nc.sync.dma_start(key_list[:], offs)
+        nc.sync.dma_start(kb_pool[DATA_ROW : DATA_ROW + 1, :], kb[0:1, :])
         nc.sync.dma_start(value_list[:], voffs)
         nc.sync.dma_start(qw[:], q_words[0, 0].rearrange("p q r -> p (q r)").bitcast(I32))
         nc.sync.dma_start(kw_pool[:], k_words[0].rearrange("p t r -> p (t r)").bitcast(I32))
-        nc.scalar.dma_start(kb_pool[DATA_ROW : DATA_ROW + 1, :], kb[0:1, :])
         for g in range(QUADRANTS):
             nc.scalar.dma_start(ks_pool[32 * g : 32 * g + 4, :].bitcast(I32), k_scales[0, 4 * g : 4 * g + 4, :].bitcast(I32))
-        nc.scalar.activation(warm[:], ident[:, 0:1], ACT.Tanh)
+        nc.scalar.activation(warm[:, 1:2], warm[:, 0:1], ACT.Tanh)
         for g in range(QUADRANTS):
             nc.scalar.dma_start(qs[32 * g : 32 * g + 4, :].bitcast(I32), q_scales[0, 0, 4 * g : 4 * g + 4, :].bitcast(I32))
-        for g in range(QUADRANTS):
-            nc.sync.dma_start(
-                vsc_pool[32 * g : 32 * g + 4, :].bitcast(I32).rearrange("p (u e) -> p u e", u=POOL_PAGES),
-                v_scales[:, 4 * g : 4 * g + 4, :].rearrange("u f e -> f u e").bitcast(I32),
-            )
 
         def page_list(e):
             cols = PAGE // LIST_ROWS
@@ -88,37 +88,51 @@ def tile_attend_pkv8q_rel2_cap_kb_kernel(
             for t in range(PACK):
                 nc.tensor.transpose(dst[:, t, :], row[:, t:PAGE:PACK], ident[:])
 
+        kb_row = sb([P, N], F32, "kb_row", "b")
+        cols = PAGE // LIST_ROWS
+        nc.vector.tensor_copy(kb_row[:, 0:PAGE], kb_pool[:].indirect(key_list[:, 0:cols]))
+        nc.vector.tensor_copy(kb_row[:, PAGE:N], kb_pool[:].indirect(key_list[:, cols : 3 * cols]))
         kb_col = []
         for e in range(PAGES):
-            row = sb([P, PAGE], F32, "kb_row%d" % e, "abf"[e])
-            nc.vector.tensor_copy(row[:], kb_pool[:].indirect(page_list(e)))
             turned = bank("kb_t%d" % e, "p%d" % e)
-            turn(turned, row)
+            turn(turned, kb_row[:, page(e)])
             col = sb([P, PACK], F32, "kb_col%d" % e)
             nc.scalar.copy(col[:], turned[:, :, DATA_ROW])
             kb_col.append(col)
 
-        vw_pool = sb([P, POOL_PAGES * DV], I32, "vw_pool", "a")
+        vs_pool = sb([P, T], F32, "vs_pool", "a")
+        nc.sync.dma_start(vs_pool[:], vs)
+        vw_pool = sb([P, POOL_PAGES * DV], I32, "vw_pool", "b")
         nc.sync.dma_start(
             vw_pool[:].rearrange("p (u e) -> p u e", u=POOL_PAGES),
             v_words.rearrange("u p e r -> p u (e r)").bitcast(I32),
         )
-        vs_pool = sb([P, T], F32, "vs_pool", "b")
-        nc.sync.dma_start(vs_pool[:], vs)
+        for g in range(QUADRANTS):
+            nc.sync.dma_start(
+                vsc_pool[32 * g : 32 * g + 4, :].bitcast(I32).rearrange("p (u e) -> p u e", u=POOL_PAGES),
+                v_scales[:, 4 * g : 4 * g + 4, :].rearrange("u f e -> f u e").bitcast(I32),
+            )
 
-        ks = sb([P, N], U8, "ks")
-        for e in range(PAGES):
-            nc.vector.tensor_copy(ks[:, page(e)], ks_pool[:].indirect(page_list(e)))
-        kw = sb([P, N], U32, "kw", "c")
-        for e in range(PAGES):
-            nc.vector.tensor_copy(kw[:, page(e)], kw_pool[:].bitcast(U32).indirect(page_list(e)))
+        ks, kw = {}, {}
+
+        def gather_scales(e, tag):
+            ks[e] = sb([P, PAGE], U8, "ks%d" % e, tag)
+            nc.vector.tensor_copy(ks[e][:], ks_pool[:].indirect(page_list(e)))
+
+        def gather_keys(e, tag):
+            kw[e] = sb([P, PAGE], U32, "kw%d" % e, tag)
+            nc.vector.tensor_copy(kw[e][:], kw_pool[:].bitcast(U32).indirect(page_list(e)))
+
+        gather_scales(0, "s0")
+        gather_keys(0, "s2")
+        gather_scales(1, "s1")
 
         def score(e, tag, tag_t):
             scores = bank("scores%d" % e, tag)
             flat = scores[:].rearrange("q t s -> q (t s)")
             nc.tensor.matmul_mx(
-                flat, lhsT=qw[:].bitcast(FP8X4), lhsT_scale=qs[:], rhs=kw[:, page(e)].bitcast(FP8X4),
-                rhs_scale=ks[:, page(e)], start=True, stop=True,
+                flat, lhsT=qw[:].bitcast(FP8X4), lhsT_scale=qs[:], rhs=kw[e][:].bitcast(FP8X4),
+                rhs_scale=ks[e][:], start=True, stop=True,
             )
             dealt = sb([P, PACK, P], F32, "dealt%d" % e)
             nc.scalar.copy(dealt[:], flat.rearrange("q (s t) -> q t s", t=PACK))
@@ -141,24 +155,28 @@ def tile_attend_pkv8q_rel2_cap_kb_kernel(
             return p
 
         st0 = score(0, "p0", "p2")
+        gather_keys(1, "s0")
+        gather_scales(2, "s2")
         st1 = score(1, "p1", "p0")
+        gather_keys(2, "s1")
         pos0 = positive(0, st0)
         st2 = score(2, "p2", "p1")
         p_t = [weigh(0, pos0)]
         p_t.append(weigh(1, positive(1, st1)))
         p_t.append(weigh(2, positive(2, st2)))
 
-        vw = sb([P, PAGES * DV], U32, "vw", "d")
-        nc.vector.tensor_copy(vw[:], vw_pool[:].bitcast(U32).indirect(value_list[:]))
-        vsc = sb([P, PAGES * DV], U8, "vsc", "a")
-        nc.vector.tensor_copy(vsc[:], vsc_pool[:].indirect(value_list[:]))
-        vs_row = sb([P, N], F32, "vs_row", "e")
+        vs_row = sb([P, N], F32, "vs_row", "d")
+        nc.vector.tensor_copy(vs_row[:, 0 : 2 * PAGE], vs_pool[:].indirect(key_list[:, 0 : 2 * cols]))
+        nc.vector.tensor_copy(vs_row[:, 2 * PAGE : N], vs_pool[:].indirect(key_list[:, 2 * cols : 3 * cols]))
         vs_t = []
         for e in range(PAGES):
-            nc.vector.tensor_copy(vs_row[:, page(e)], vs_pool[:].indirect(page_list(e)))
             turned = bank("vs_t%d" % e, ("p2", "p0", "p1")[e])
             turn(turned, vs_row[:, page(e)])
             vs_t.append(turned)
+        vw = sb([P, PAGES * DV], U32, "vw", "a")
+        nc.vector.tensor_copy(vw[:], vw_pool[:].bitcast(U32).indirect(value_list[:]))
+        vsc = sb([P, PAGES * DV], U8, "vsc", "b")
+        nc.vector.tensor_copy(vsc[:], vsc_pool[:].indirect(value_list[:]))
 
         total = psum.tile([P, P], F32, name="total")
         acc = psum.tile([P, DV], F32, name="acc")
@@ -171,9 +189,9 @@ def tile_attend_pkv8q_rel2_cap_kb_kernel(
                 )
             w = sb([P, NQ * PACK], BF16, "w%d" % e)
             nc.vector.tensor_tensor(
-                w[:].rearrange("s (c i t) -> s c t i", i=4, t=PACK),
-                p[:].rearrange("s t (c i) -> s c t i", i=4),
-                vs_t[e][:].rearrange("s t (c i) -> s c t i", i=4),
+                w[:].rearrange("s (c i t) -> s c t i", i=2, t=PACK),
+                p[:].rearrange("s t (c i) -> s c t i", i=2),
+                vs_t[e][:].rearrange("s t (c i) -> s c t i", i=2),
                 ALU.mult,
             )
             w_codes = sb([P, NQ], U32, "w_codes%d" % e)

@@ -49,7 +49,7 @@ def tile_attend_pkv8q_rel2_cap_kb_kernel(
         kw_pool = sb([P, T], I32, "kw_pool", "d")
         ks_pool = sb([P, T], U8, "ks_pool")
         vsc_pool = sb([P, POOL_PAGES * DV], U8, "vsc_pool")
-        kb_pool = sb([P, T], F32, "kb_pool", "a")
+        kb_pool = sb([P, T], F32, "kb_pool")
         qw = sb([P, NQ], I32, "qw")
         qs = sb([P, NQ], U8, "qs")
         ident = sb([P, P], F32, "ident")
@@ -88,25 +88,22 @@ def tile_attend_pkv8q_rel2_cap_kb_kernel(
             for t in range(PACK):
                 nc.tensor.transpose(dst[:, t, :], row[:, t:PAGE:PACK], ident[:])
 
-        kb_row = sb([P, N], F32, "kb_row", "b")
         cols = PAGE // LIST_ROWS
-        nc.vector.tensor_copy(kb_row[:, 0:PAGE], kb_pool[:].indirect(key_list[:, 0:cols]))
-        nc.vector.tensor_copy(kb_row[:, PAGE:N], kb_pool[:].indirect(key_list[:, cols : 3 * cols]))
-        kb_col = []
-        for e in range(PAGES):
-            turned = bank("kb_t%d" % e, "p%d" % e)
-            turn(turned, kb_row[:, page(e)])
-            col = sb([P, PACK], F32, "kb_col%d" % e)
-            nc.scalar.copy(col[:], turned[:, :, DATA_ROW])
-            kb_col.append(col)
+        kb_col = {}
+
+        def bias_column(e, row, tag):
+            turned = bank("kb_t%d" % e, tag)
+            turn(turned, row)
+            kb_col[e] = sb([P, PACK], F32, "kb_col%d" % e)
+            nc.scalar.copy(kb_col[e][:], turned[:, :, DATA_ROW])
+
+        for e, tag in ((0, "a"), (1, None)):
+            kb_row = sb([P, PAGE], F32, "kb_row%d" % e, tag)
+            nc.vector.tensor_copy(kb_row[:], kb_pool[:].indirect(page_list(e)))
+            bias_column(e, kb_row[:], "xy"[e])
 
         vs_pool = sb([P, T], F32, "vs_pool", "a")
         nc.sync.dma_start(vs_pool[:], vs)
-        vw_pool = sb([P, POOL_PAGES * DV], I32, "vw_pool", "b")
-        nc.sync.dma_start(
-            vw_pool[:].rearrange("p (u e) -> p u e", u=POOL_PAGES),
-            v_words.rearrange("u p e r -> p u (e r)").bitcast(I32),
-        )
         for g in range(QUADRANTS):
             nc.sync.dma_start(
                 vsc_pool[32 * g : 32 * g + 4, :].bitcast(I32).rearrange("p (u e) -> p u e", u=POOL_PAGES),
@@ -124,8 +121,9 @@ def tile_attend_pkv8q_rel2_cap_kb_kernel(
             nc.vector.tensor_copy(kw[e][:], kw_pool[:].bitcast(U32).indirect(page_list(e)))
 
         gather_scales(0, "s0")
-        gather_keys(0, "s2")
         gather_scales(1, "s1")
+        gather_keys(0, "s2")
+        gather_keys(1, "b")
 
         def score(e, tag, tag_t):
             scores = bank("scores%d" % e, tag)
@@ -154,13 +152,20 @@ def tile_attend_pkv8q_rel2_cap_kb_kernel(
             nc.scalar.activation(p[:], capped[:], ACT.Square, scale=CAP)
             return p
 
-        st0 = score(0, "p0", "p2")
-        gather_keys(1, "s0")
+        st0 = score(0, "w", "x")
+        kb_row2 = sb([P, PAGE], F32, "kb_row2", "s0")
+        nc.vector.tensor_copy(kb_row2[:], kb_pool[:].indirect(page_list(2)))
         gather_scales(2, "s2")
-        st1 = score(1, "p1", "p0")
+        st1 = score(1, "u", "w")
         gather_keys(2, "s1")
+        vw_pool = sb([P, POOL_PAGES * DV], I32, "vw_pool", "b")
+        nc.sync.dma_start(
+            vw_pool[:].rearrange("p (u e) -> p u e", u=POOL_PAGES),
+            v_words.rearrange("u p e r -> p u (e r)").bitcast(I32),
+        )
         pos0 = positive(0, st0)
-        st2 = score(2, "p2", "p1")
+        bias_column(2, kb_row2[:], "u")
+        st2 = score(2, "x", "y")
         p_t = [weigh(0, pos0)]
         p_t.append(weigh(1, positive(1, st1)))
         p_t.append(weigh(2, positive(2, st2)))
@@ -170,7 +175,7 @@ def tile_attend_pkv8q_rel2_cap_kb_kernel(
         nc.vector.tensor_copy(vs_row[:, 2 * PAGE : N], vs_pool[:].indirect(key_list[:, 2 * cols : 3 * cols]))
         vs_t = []
         for e in range(PAGES):
-            turned = bank("vs_t%d" % e, ("p2", "p0", "p1")[e])
+            turned = bank("vs_t%d" % e, "xwy"[e])
             turn(turned, vs_row[:, page(e)])
             vs_t.append(turned)
         vw = sb([P, PAGES * DV], U32, "vw", "a")
@@ -180,33 +185,43 @@ def tile_attend_pkv8q_rel2_cap_kb_kernel(
 
         total = psum.tile([P, P], F32, name="total")
         acc = psum.tile([P, DV], F32, name="acc")
+        nc.tensor.matmul(total[:], lhsT=ident[:], rhs=ident[:], is_transpose=True, start=True, stop=False)
         for e in range(PAGES):
-            p = p_t[e]
             for t in range(PACK):
                 nc.tensor.matmul(
-                    total[:], lhsT=p[:, t, :], rhs=ident[:], is_transpose=True,
-                    start=(e == 0 and t == 0), stop=(e == PAGES - 1 and t == PACK - 1),
+                    total[:], lhsT=p_t[e][:, t, :], rhs=ident[:], is_transpose=True,
+                    start=False, stop=(e == PAGES - 1 and t == PACK - 1),
                 )
-            w = sb([P, NQ * PACK], BF16, "w%d" % e)
+        parts = sb([P, P], F32, "parts")
+        denom = sb([P, 1], F32, "denom")
+        nc.scalar.activation(parts[:], total[:], ACT.Copy, accum_out=denom[:])
+
+        w = [sb([P, NQ * PACK], BF16, "w%d" % e) for e in range(PAGES)]
+        vs_col = sb([P, PACK], F32, "vs_col")
+        nc.scalar.copy(vs_col[:], vs_t[0][:, :, 0])
+        w_planes = sb([P, PACK, NQ], BF16, "w_planes")
+        for t in range(PACK):
+            nc.scalar.activation(w_planes[:, t, :], p_t[0][:, t, :], ACT.Copy, scale=vs_col[:, t : t + 1])
+        nc.scalar.copy(w[0][:].rearrange("s (q t) -> s q t", t=PACK), w_planes[:].rearrange("s t q -> s q t"))
+        for e in (1, 2):
             nc.vector.tensor_tensor(
-                w[:].rearrange("s (c i t) -> s c t i", i=2, t=PACK),
-                p[:].rearrange("s t (c i) -> s c t i", i=2),
+                w[e][:].rearrange("s (c i t) -> s c t i", i=2, t=PACK),
+                p_t[e][:].rearrange("s t (c i) -> s c t i", i=2),
                 vs_t[e][:].rearrange("s t (c i) -> s c t i", i=2),
                 ALU.mult,
             )
+        order = (1, 0, 2)
+        for e in order:
             w_codes = sb([P, NQ], U32, "w_codes%d" % e)
             w_scales = sb([P, NQ], U8, "w_scales%d" % e)
-            nc.vector.quantize_mx(w_codes[:].bitcast(FP8X4), w_scales[:], w[:])
+            nc.vector.quantize_mx(w_codes[:].bitcast(FP8X4), w_scales[:], w[e][:])
             cols = slice(e * DV, (e + 1) * DV)
             nc.tensor.matmul_mx(
                 acc[:], lhsT=w_codes[:].bitcast(FP8X4), lhsT_scale=w_scales[:],
                 rhs=vw[:, cols].bitcast(FP8X4), rhs_scale=vsc[:, cols],
-                start=(e == 0), stop=(e == PAGES - 1),
+                start=(e == order[0]), stop=(e == order[-1]),
             )
 
-        parts = sb([P, P], F32, "parts")
-        denom = sb([P, 1], F32, "denom")
-        nc.vector.tensor_scalar(parts[:], total[:], 1.0, 1.0, op0=ALU.mult, op1=ALU.add, accum_out=denom[:])
         inv = sb([P, 1], F32, "inv")
         nc.vector.reciprocal(inv[:], denom[:])
         y = sb([P, DV], F32, "y")

@@ -56,12 +56,13 @@ def tile_attend_pkv8q_rel2_cap_kb_kernel(
         warm = sb([P, 2], F32, "warm")
 
         ks_words = ks_pool[:].bitcast(I32)
+        nc.gpsimd.memset(ks_words[:, 0:640], 0)
+        nc.vector.memset(ks_words[:, 640:895], 0)
+        nc.vector.memset(ks_words[:, 895:1024], 0)
+        nc.vector.memset(kb_pool[0:DATA_ROW, 0:935], 0.0)
+        nc.vector.memset(kb_pool[0:DATA_ROW, 935:1872], 0.0)
+        nc.gpsimd.memset(kb_pool[0:DATA_ROW, 1872:T], 0.0)
         nc.gpsimd.memset(warm[:, 0:1], 0.0)
-        nc.vector.memset(ks_words[:, 0:511], 0)
-        nc.vector.memset(ks_words[:, 511:1024], 0)
-        nc.vector.memset(kb_pool[0:DATA_ROW, 0:615], 0.0)
-        nc.vector.memset(kb_pool[0:DATA_ROW, 615:1232], 0.0)
-        nc.gpsimd.memset(kb_pool[0:DATA_ROW, 1232:T], 0.0)
         nc.gpsimd.memset(qs[:].bitcast(I32), 0)
         make_identity(nc, ident[:])
         nc.gpsimd.memset(vsc_pool[:].bitcast(I32), 0)
@@ -75,7 +76,8 @@ def tile_attend_pkv8q_rel2_cap_kb_kernel(
             nc.scalar.dma_start(ks_pool[32 * g : 32 * g + 4, :].bitcast(I32), k_scales[0, 4 * g : 4 * g + 4, :].bitcast(I32))
         nc.scalar.activation(warm[:, 1:2], warm[:, 0:1], ACT.Tanh)
         for g in range(QUADRANTS):
-            nc.scalar.dma_start(qs[32 * g : 32 * g + 4, :].bitcast(I32), q_scales[0, 0, 4 * g : 4 * g + 4, :].bitcast(I32))
+            queue = nc.gpsimd if g == QUADRANTS - 1 else nc.scalar
+            queue.dma_start(qs[32 * g : 32 * g + 4, :].bitcast(I32), q_scales[0, 0, 4 * g : 4 * g + 4, :].bitcast(I32))
 
         def page_list(e):
             cols = PAGE // LIST_ROWS
@@ -105,7 +107,7 @@ def tile_attend_pkv8q_rel2_cap_kb_kernel(
         vs_pool = sb([P, T], F32, "vs_pool", "a")
         nc.sync.dma_start(vs_pool[:], vs)
         for g in range(QUADRANTS):
-            nc.sync.dma_start(
+            nc.scalar.dma_start(
                 vsc_pool[32 * g : 32 * g + 4, :].bitcast(I32).rearrange("p (u e) -> p u e", u=POOL_PAGES),
                 v_scales[:, 4 * g : 4 * g + 4, :].rearrange("u f e -> f u e").bitcast(I32),
             )
@@ -121,9 +123,8 @@ def tile_attend_pkv8q_rel2_cap_kb_kernel(
             nc.vector.tensor_copy(kw[e][:], kw_pool[:].bitcast(U32).indirect(page_list(e)))
 
         gather_scales(0, "s0")
-        gather_scales(1, "s1")
-        gather_keys(0, "s2")
-        gather_keys(1, "b")
+        gather_keys(0, "b")
+        gather_keys(1, "s1")
 
         def score(e, tag, tag_t):
             scores = bank("scores%d" % e, tag)
@@ -153,18 +154,19 @@ def tile_attend_pkv8q_rel2_cap_kb_kernel(
             return p
 
         st0 = score(0, "w", "x")
-        kb_row2 = sb([P, PAGE], F32, "kb_row2", "s0")
+        gather_scales(1, "s0")
+        kb_row2 = sb([P, PAGE], F32, "kb_row2", "b")
         nc.vector.tensor_copy(kb_row2[:], kb_pool[:].indirect(page_list(2)))
-        gather_scales(2, "s2")
         st1 = score(1, "u", "w")
+        gather_scales(2, "s0")
         gather_keys(2, "s1")
+        pos0 = positive(0, st0)
+        bias_column(2, kb_row2[:], "u")
         vw_pool = sb([P, POOL_PAGES * DV], I32, "vw_pool", "b")
         nc.sync.dma_start(
             vw_pool[:].rearrange("p (u e) -> p u e", u=POOL_PAGES),
             v_words.rearrange("u p e r -> p u (e r)").bitcast(I32),
         )
-        pos0 = positive(0, st0)
-        bias_column(2, kb_row2[:], "u")
         st2 = score(2, "x", "y")
         p_t = [weigh(0, pos0)]
         p_t.append(weigh(1, positive(1, st1)))

@@ -12,10 +12,14 @@ P = 128
 PACK = 4
 QUADRANTS = 4
 LIST_ROWS = 16
-DATA_ROW = 127
+BIAS_ROW = P - 1
+PAIR = 2
+
+KS_SPLIT = (640, 895)
+KB_SPLIT = (935, 1872)
 
 FLOPS = 2 * NQ * N * D + 2 * NQ * N * DV
-BYTES = T * D + T * D // 32 + T * DV + T * DV // 32 + NQ * D + NQ * D // 32 + 2 * 4 * T + 2 * P * (N + PAGES * DV) // LIST_ROWS + 4 * NQ * DV
+BYTES = (T * D + T * DV + NQ * D) * 33 // 32 + 2 * 4 * T + 2 * P * (N + PAGES * DV) // LIST_ROWS + 4 * NQ * DV
 
 F32 = mybir.dt.float32
 BF16 = mybir.dt.bfloat16
@@ -37,47 +41,46 @@ def tile_attend_pkv8q_rel2_cap_kb_kernel(
         held = ctx.enter_context(tc.tile_pool(name="held", bufs=1))
         psum = ctx.enter_context(tc.psum_pool(name="psum", bufs=1))
 
-        key_list = lists.tile([P, N // LIST_ROWS], U16, name="key_list")
-        value_list = lists.tile([P, PAGES * DV // LIST_ROWS], U16, name="value_list")
-
         def sb(shape, dtype, name, tag=None):
             return held.tile(shape, dtype, name=name, tag=tag or name, align_bytes=64)
 
         def bank(name, tag):
             return psum.tile([P, PACK, P], F32, name=name, tag=tag)
 
-        kw_pool = sb([P, T], I32, "kw_pool", "d")
+        def scale_rows(plane, g):
+            return plane[32 * g : 32 * g + 4, :].bitcast(I32)
+
+        key_list = lists.tile([P, N // LIST_ROWS], U16, name="key_list")
+        value_list = lists.tile([P, PAGES * DV // LIST_ROWS], U16, name="value_list")
+        kw_pool = sb([P, T], I32, "kw_pool", "keys_then_vs_row")
         ks_pool = sb([P, T], U8, "ks_pool")
         vsc_pool = sb([P, POOL_PAGES * DV], U8, "vsc_pool")
-        kb_pool = sb([P, T], F32, "kb_pool")
+        kb_pool = sb([P, T], F32, "kb_pool", "kb_then_vs_then_vw")
         qw = sb([P, NQ], I32, "qw")
         qs = sb([P, NQ], U8, "qs")
         ident = sb([P, P], F32, "ident")
-        warm = sb([P, 2], F32, "warm")
 
         ks_words = ks_pool[:].bitcast(I32)
-        nc.gpsimd.memset(ks_words[:, 0:640], 0)
-        nc.vector.memset(ks_words[:, 640:895], 0)
-        nc.vector.memset(ks_words[:, 895:1024], 0)
-        nc.vector.memset(kb_pool[0:DATA_ROW, 0:935], 0.0)
-        nc.vector.memset(kb_pool[0:DATA_ROW, 935:1872], 0.0)
-        nc.gpsimd.memset(kb_pool[0:DATA_ROW, 1872:T], 0.0)
-        nc.gpsimd.memset(warm[:, 0:1], 0.0)
+        nc.gpsimd.memset(ks_words[:, 0 : KS_SPLIT[0]], 0)
+        nc.vector.memset(ks_words[:, KS_SPLIT[0] : KS_SPLIT[1]], 0)
+        nc.vector.memset(ks_words[:, KS_SPLIT[1] : T // 4], 0)
+        nc.vector.memset(kb_pool[0:BIAS_ROW, 0 : KB_SPLIT[0]], 0.0)
+        nc.vector.memset(kb_pool[0:BIAS_ROW, KB_SPLIT[0] : KB_SPLIT[1]], 0.0)
+        nc.gpsimd.memset(kb_pool[0:BIAS_ROW, KB_SPLIT[1] : T], 0.0)
         nc.gpsimd.memset(qs[:].bitcast(I32), 0)
         make_identity(nc, ident[:])
         nc.gpsimd.memset(vsc_pool[:].bitcast(I32), 0)
 
         nc.sync.dma_start(key_list[:], offs)
-        nc.sync.dma_start(kb_pool[DATA_ROW : DATA_ROW + 1, :], kb[0:1, :])
+        nc.sync.dma_start(kb_pool[BIAS_ROW:P, :], kb[0:1, :])
         nc.sync.dma_start(value_list[:], voffs)
         nc.sync.dma_start(qw[:], q_words[0, 0].rearrange("p q r -> p (q r)").bitcast(I32))
         nc.sync.dma_start(kw_pool[:], k_words[0].rearrange("p t r -> p (t r)").bitcast(I32))
         for g in range(QUADRANTS):
-            nc.scalar.dma_start(ks_pool[32 * g : 32 * g + 4, :].bitcast(I32), k_scales[0, 4 * g : 4 * g + 4, :].bitcast(I32))
-        nc.scalar.activation(warm[:, 1:2], warm[:, 0:1], ACT.Tanh)
+            nc.scalar.dma_start(scale_rows(ks_pool, g), k_scales[0, 4 * g : 4 * g + 4, :].bitcast(I32))
         for g in range(QUADRANTS):
             queue = nc.gpsimd if g == QUADRANTS - 1 else nc.scalar
-            queue.dma_start(qs[32 * g : 32 * g + 4, :].bitcast(I32), q_scales[0, 0, 4 * g : 4 * g + 4, :].bitcast(I32))
+            queue.dma_start(scale_rows(qs, g), q_scales[0, 0, 4 * g : 4 * g + 4, :].bitcast(I32))
 
         def page_list(e):
             cols = PAGE // LIST_ROWS
@@ -86,103 +89,91 @@ def tile_attend_pkv8q_rel2_cap_kb_kernel(
         def page(e):
             return slice(e * PAGE, (e + 1) * PAGE)
 
-        def turn(dst, row):
+        def turn(name, row, copy, bank_tag):
+            planes = sb([P, PACK, P], F32, name + "_planes")
+            copy(planes[:].rearrange("p t s -> p s t"), row.rearrange("p (s t) -> p s t", t=PACK))
+            turned = bank(name + "_t", bank_tag)
             for t in range(PACK):
-                nc.tensor.transpose(dst[:, t, :], row[:, t:PAGE:PACK], ident[:])
+                nc.tensor.transpose(turned[:, t, :], planes[:, t, :], ident[:])
+            return turned
 
-        cols = PAGE // LIST_ROWS
-        kb_col = {}
+        kb_row = sb([P, N], F32, "kb_row", "kb_row_then_values")
+        nc.vector.tensor_copy(kb_row[:], kb_pool[:].indirect(key_list[:]))
+        kb_col = []
+        for e in range(PAGES):
+            turned = turn("kb%d" % e, kb_row[:, page(e)], nc.scalar.copy, "bank%d" % e)
+            col = sb([P, PACK], F32, "kb_col%d" % e)
+            nc.scalar.copy(col[:], turned[:, :, BIAS_ROW])
+            kb_col.append(col)
 
-        def bias_column(e, row, tag):
-            turned = bank("kb_t%d" % e, tag)
-            turn(turned, row)
-            kb_col[e] = sb([P, PACK], F32, "kb_col%d" % e)
-            nc.scalar.copy(kb_col[e][:], turned[:, :, DATA_ROW])
-
-        for e, tag in ((0, "a"), (1, None)):
-            kb_row = sb([P, PAGE], F32, "kb_row%d" % e, tag)
-            nc.vector.tensor_copy(kb_row[:], kb_pool[:].indirect(page_list(e)))
-            bias_column(e, kb_row[:], "xy"[e])
-
-        vs_pool = sb([P, T], F32, "vs_pool", "a")
+        vs_pool = sb([P, T], F32, "vs_pool", "kb_then_vs_then_vw")
         nc.sync.dma_start(vs_pool[:], vs)
+        vw_pool = sb([P, POOL_PAGES * DV], I32, "vw_pool", "kb_row_then_values")
+        nc.sync.dma_start(
+            vw_pool[:].rearrange("p (u e) -> p u e", u=POOL_PAGES),
+            v_words.rearrange("u p e r -> p u (e r)").bitcast(I32),
+        )
         for g in range(QUADRANTS):
             nc.scalar.dma_start(
-                vsc_pool[32 * g : 32 * g + 4, :].bitcast(I32).rearrange("p (u e) -> p u e", u=POOL_PAGES),
+                scale_rows(vsc_pool, g).rearrange("p (u e) -> p u e", u=POOL_PAGES),
                 v_scales[:, 4 * g : 4 * g + 4, :].rearrange("u f e -> f u e").bitcast(I32),
             )
 
         ks, kw = {}, {}
 
-        def gather_scales(e, tag):
+        def gather_key_scales(e, tag):
             ks[e] = sb([P, PAGE], U8, "ks%d" % e, tag)
             nc.vector.tensor_copy(ks[e][:], ks_pool[:].indirect(page_list(e)))
 
-        def gather_keys(e, tag):
+        def gather_key_words(e, tag=None):
             kw[e] = sb([P, PAGE], U32, "kw%d" % e, tag)
             nc.vector.tensor_copy(kw[e][:], kw_pool[:].bitcast(U32).indirect(page_list(e)))
 
-        gather_scales(0, "s0")
-        gather_keys(0, "b")
-        gather_keys(1, "s1")
+        gather_key_scales(0, "ks0_then_ks2")
+        gather_key_scales(1, "ks1_then_kw2")
+        gather_key_words(0)
+        gather_key_words(1)
 
-        def score(e, tag, tag_t):
-            scores = bank("scores%d" % e, tag)
+        def score(e, bank_tag, turned_tag):
+            scores = bank("scores%d" % e, bank_tag)
             flat = scores[:].rearrange("q t s -> q (t s)")
             nc.tensor.matmul_mx(
                 flat, lhsT=qw[:].bitcast(FP8X4), lhsT_scale=qs[:], rhs=kw[e][:].bitcast(FP8X4),
                 rhs_scale=ks[e][:], start=True, stop=True,
             )
-            dealt = sb([P, PACK, P], F32, "dealt%d" % e)
-            nc.scalar.copy(dealt[:], flat.rearrange("q (s t) -> q t s", t=PACK))
-            scores_t = bank("scores_t%d" % e, tag_t)
+            planes = sb([P, PACK, P], F32, "score_planes%d" % e)
+            nc.scalar.copy(planes[:], flat.rearrange("q (s t) -> q t s", t=PACK))
+            scores_t = bank("scores_t%d" % e, turned_tag)
             for t in range(PACK):
-                nc.tensor.transpose(scores_t[:, t, :], dealt[:, t, :], ident[:])
+                nc.tensor.transpose(scores_t[:, t, :], planes[:, t, :], ident[:])
             return scores_t
 
-        def positive(e, scores_t):
+        def weigh(e, scores_t):
             pos = sb([P, PACK, NQ], F32, "pos%d" % e)
             for t in range(PACK):
                 nc.scalar.activation(pos[:, t, :], scores_t[:, t, :], ACT.Relu, bias=kb_col[e][:, t : t + 1])
-            return pos
-
-        def weigh(e, pos):
             capped = sb([P, PACK, NQ], F32, "capped%d" % e)
             nc.scalar.activation(capped[:], pos[:], ACT.Tanh, scale=1.0 / CAP)
             p = sb([P, PACK, NQ], F32, "p%d" % e)
             nc.scalar.activation(p[:], capped[:], ACT.Square, scale=CAP)
             return p
 
-        st0 = score(0, "w", "x")
-        gather_scales(1, "s0")
-        kb_row2 = sb([P, PAGE], F32, "kb_row2", "b")
-        nc.vector.tensor_copy(kb_row2[:], kb_pool[:].indirect(page_list(2)))
-        st1 = score(1, "u", "w")
-        gather_scales(2, "s0")
-        gather_keys(2, "s1")
-        pos0 = positive(0, st0)
-        bias_column(2, kb_row2[:], "u")
-        vw_pool = sb([P, POOL_PAGES * DV], I32, "vw_pool", "b")
-        nc.sync.dma_start(
-            vw_pool[:].rearrange("p (u e) -> p u e", u=POOL_PAGES),
-            v_words.rearrange("u p e r -> p u (e r)").bitcast(I32),
-        )
-        st2 = score(2, "x", "y")
-        p_t = [weigh(0, pos0)]
-        p_t.append(weigh(1, positive(1, st1)))
-        p_t.append(weigh(2, positive(2, st2)))
+        scores_t0 = score(0, "bank0", "bank2")
+        gather_key_scales(2, "ks0_then_ks2")
+        scores_t1 = score(1, "bank1", "bank0")
+        gather_key_words(2, "ks1_then_kw2")
+        p_t = [weigh(0, scores_t0)]
+        p_t.append(weigh(1, scores_t1))
+        p_t.append(weigh(2, score(2, "bank0", "bank1")))
 
-        vs_row = sb([P, N], F32, "vs_row", "d")
-        nc.vector.tensor_copy(vs_row[:, 0 : 2 * PAGE], vs_pool[:].indirect(key_list[:, 0 : 2 * cols]))
-        nc.vector.tensor_copy(vs_row[:, 2 * PAGE : N], vs_pool[:].indirect(key_list[:, 2 * cols : 3 * cols]))
-        vs_t = []
+        vs_row = sb([P, N], F32, "vs_row", "keys_then_vs_row")
         for e in range(PAGES):
-            turned = bank("vs_t%d" % e, "xwy"[e])
-            turn(turned, vs_row[:, page(e)])
-            vs_t.append(turned)
-        vw = sb([P, PAGES * DV], U32, "vw", "a")
+            nc.vector.tensor_copy(vs_row[:, page(e)], vs_pool[:].indirect(page_list(e)))
+        vs_banks = ("bank2", "bank0", "bank1")
+        vs_t = [turn("vs%d" % e, vs_row[:, page(e)], nc.vector.tensor_copy, vs_banks[e]) for e in range(PAGES)]
+        vw = sb([P, PAGES * DV], U32, "vw", "kb_then_vs_then_vw")
         nc.vector.tensor_copy(vw[:], vw_pool[:].bitcast(U32).indirect(value_list[:]))
-        vsc = sb([P, PAGES * DV], U8, "vsc", "b")
+        vsc = sb([P, PAGES * DV], U8, "vsc", "kb_row_then_values")
         nc.vector.tensor_copy(vsc[:], vsc_pool[:].indirect(value_list[:]))
 
         total = psum.tile([P, P], F32, name="total")
@@ -205,13 +196,14 @@ def tile_attend_pkv8q_rel2_cap_kb_kernel(
         for t in range(PACK):
             nc.scalar.activation(w_planes[:, t, :], p_t[0][:, t, :], ACT.Copy, scale=vs_col[:, t : t + 1])
         nc.scalar.copy(w[0][:].rearrange("s (q t) -> s q t", t=PACK), w_planes[:].rearrange("s t q -> s q t"))
-        for e in (1, 2):
+        for e in range(1, PAGES):
             nc.vector.tensor_tensor(
-                w[e][:].rearrange("s (c i t) -> s c t i", i=2, t=PACK),
-                p_t[e][:].rearrange("s t (c i) -> s c t i", i=2),
-                vs_t[e][:].rearrange("s t (c i) -> s c t i", i=2),
+                w[e][:].rearrange("s (c i t) -> s c t i", i=PAIR, t=PACK),
+                p_t[e][:].rearrange("s t (c i) -> s c t i", i=PAIR),
+                vs_t[e][:].rearrange("s t (c i) -> s c t i", i=PAIR),
                 ALU.mult,
             )
+
         order = (1, 0, 2)
         for e in order:
             w_codes = sb([P, NQ], U32, "w_codes%d" % e)

@@ -39,10 +39,14 @@ def tile_attend_pkv8q_rel2_cap_kb_kernel(
     with ExitStack() as ctx:
         lists = ctx.enter_context(tc.tile_pool(name="lists", bufs=1))
         held = ctx.enter_context(tc.tile_pool(name="held", bufs=1))
+        placed = ctx.enter_context(tc.tile_pool(name="placed", bufs=1))
         psum = ctx.enter_context(tc.psum_pool(name="psum", bufs=1))
 
         def sb(shape, dtype, name, tag=None):
             return held.tile(shape, dtype, name=name, tag=tag or name, align_bytes=64)
+
+        def at(offset, shape, dtype, name):
+            return placed.tile(shape, dtype, name=name, align_bytes=64, offset=offset)
 
         def bank(name, tag):
             return psum.tile([P, PACK, P], F32, name=name, tag=tag)
@@ -52,10 +56,10 @@ def tile_attend_pkv8q_rel2_cap_kb_kernel(
 
         key_list = lists.tile([P, N // LIST_ROWS], U16, name="key_list")
         value_list = lists.tile([P, PAGES * DV // LIST_ROWS], U16, name="value_list")
-        kw_pool = sb([P, T], I32, "kw_pool", "keys_then_vs_row")
+        kw_pool = sb([P, T], I32, "kw_pool", "kw_pool_then_vs_rows")
         ks_pool = sb([P, T], U8, "ks_pool")
-        vsc_pool = sb([P, POOL_PAGES * DV], U8, "vsc_pool")
-        kb_pool = sb([P, T], F32, "kb_pool", "kb_then_vs_then_vw")
+        kb_pool = at(0, [P, T], F32, "kb_pool")
+        vs_pool = at(32768, [P, T], F32, "vs_pool")
         qw = sb([P, NQ], I32, "qw")
         qs = sb([P, NQ], U8, "qs")
         ident = sb([P, P], F32, "ident")
@@ -68,18 +72,20 @@ def tile_attend_pkv8q_rel2_cap_kb_kernel(
         nc.vector.memset(kb_pool[0:BIAS_ROW, KB_SPLIT[0] : KB_SPLIT[1]], 0.0)
         nc.gpsimd.memset(kb_pool[0:BIAS_ROW, KB_SPLIT[1] : T], 0.0)
         nc.gpsimd.memset(qs[:].bitcast(I32), 0)
-        make_identity(nc, ident[:])
-        nc.gpsimd.memset(vsc_pool[:].bitcast(I32), 0)
+        nc.gpsimd.memset(ident[:], 0.0)
+        nc.gpsimd.memset(vs_pool[0:BIAS_ROW, :], 0.0)
+        make_identity(nc, ident[:], nomemset=True)
 
         nc.sync.dma_start(key_list[:], offs)
         nc.sync.dma_start(kb_pool[BIAS_ROW:P, :], kb[0:1, :])
         nc.sync.dma_start(value_list[:], voffs)
         nc.sync.dma_start(qw[:], q_words[0, 0].rearrange("p q r -> p (q r)").bitcast(I32))
         nc.sync.dma_start(kw_pool[:], k_words[0].rearrange("p t r -> p (t r)").bitcast(I32))
+        nc.sync.dma_start(vs_pool[BIAS_ROW:P, :], vs[0:1, :])
         for g in range(QUADRANTS):
             nc.scalar.dma_start(scale_rows(ks_pool, g), k_scales[0, 4 * g : 4 * g + 4, :].bitcast(I32))
         for g in range(QUADRANTS):
-            queue = nc.gpsimd if g == QUADRANTS - 1 else nc.scalar
+            queue = nc.scalar if g < 2 else nc.sync
             queue.dma_start(scale_rows(qs, g), q_scales[0, 0, 4 * g : 4 * g + 4, :].bitcast(I32))
 
         def page_list(e):
@@ -89,95 +95,98 @@ def tile_attend_pkv8q_rel2_cap_kb_kernel(
         def page(e):
             return slice(e * PAGE, (e + 1) * PAGE)
 
-        def turn(name, row, copy, bank_tag):
-            planes = sb([P, PACK, P], F32, name + "_planes")
-            copy(planes[:].rearrange("p t s -> p s t"), row.rearrange("p (s t) -> p s t", t=PACK))
-            turned = bank(name + "_t", bank_tag)
-            for t in range(PACK):
-                nc.tensor.transpose(turned[:, t, :], planes[:, t, :], ident[:])
-            return turned
+        def column(name, row):
+            col = sb([P, PACK], F32, name)
+            nc.sync.dma_start(col[:], row)
+            return col
 
-        kb_row = sb([P, N], F32, "kb_row", "kb_row_then_values")
+        kb_row = sb([P, N], F32, "kb_row")
         nc.vector.tensor_copy(kb_row[:], kb_pool[:].indirect(key_list[:]))
-        kb_col = []
-        for e in range(PAGES):
-            turned = turn("kb%d" % e, kb_row[:, page(e)], nc.scalar.copy, "bank%d" % e)
-            col = sb([P, PACK], F32, "kb_col%d" % e)
-            nc.scalar.copy(col[:], turned[:, :, BIAS_ROW])
-            kb_col.append(col)
+        kb_col = [column("kb_col%d" % e, kb_row[BIAS_ROW:P, page(e)]) for e in range(PAGES)]
 
-        vs_pool = sb([P, T], F32, "vs_pool", "kb_then_vs_then_vw")
-        nc.sync.dma_start(vs_pool[:], vs)
-        vw_pool = sb([P, POOL_PAGES * DV], I32, "vw_pool", "kb_row_then_values")
+        vw_pool = at(0, [P, POOL_PAGES * DV], I32, "vw_pool")
         nc.sync.dma_start(
             vw_pool[:].rearrange("p (u e) -> p u e", u=POOL_PAGES),
             v_words.rearrange("u p e r -> p u (e r)").bitcast(I32),
         )
+        vsc_pool = at(4096, [P, POOL_PAGES * DV], U8, "vsc_pool")
+        nc.gpsimd.memset(vsc_pool[:].bitcast(I32), 0)
         for g in range(QUADRANTS):
-            nc.scalar.dma_start(
+            nc.sync.dma_start(
                 scale_rows(vsc_pool, g).rearrange("p (u e) -> p u e", u=POOL_PAGES),
                 v_scales[:, 4 * g : 4 * g + 4, :].rearrange("u f e -> f u e").bitcast(I32),
             )
 
+        vs_col, p_t = {}, []
+
         ks, kw = {}, {}
 
-        def gather_key_scales(e, tag):
-            ks[e] = sb([P, PAGE], U8, "ks%d" % e, tag)
-            nc.vector.tensor_copy(ks[e][:], ks_pool[:].indirect(page_list(e)))
+        def key_scales(first, count, row_at):
+            cols = PAGE // LIST_ROWS
+            row = at(row_at, [P, count * PAGE], U8, "ks_row%d" % first)
+            nc.vector.tensor_copy(row[:], ks_pool[:].indirect(key_list[:, first * cols : (first + count) * cols]))
+            return row
 
-        def gather_key_words(e, tag=None):
-            kw[e] = sb([P, PAGE], U32, "kw%d" % e, tag)
-            nc.vector.tensor_copy(kw[e][:], kw_pool[:].bitcast(U32).indirect(page_list(e)))
+        def deal(first, count, row):
+            dealt = sb([P, count, PACK, P], U8, "ks%d" % first)
+            nc.vector.tensor_copy(dealt[:], row[:].rearrange("p (e s t) -> p e t s", e=count, t=PACK))
+            for e in range(count):
+                ks[first + e] = dealt[:, e, :, :]
 
-        gather_key_scales(0, "ks0_then_ks2")
-        gather_key_scales(1, "ks1_then_kw2")
-        gather_key_words(0)
-        gather_key_words(1)
-
-        def score(e, bank_tag, turned_tag):
-            scores = bank("scores%d" % e, bank_tag)
-            flat = scores[:].rearrange("q t s -> q (t s)")
-            nc.tensor.matmul_mx(
-                flat, lhsT=qw[:].bitcast(FP8X4), lhsT_scale=qs[:], rhs=kw[e][:].bitcast(FP8X4),
-                rhs_scale=ks[e][:], start=True, stop=True,
+        def key_words(e, kw_at):
+            kw[e] = at(kw_at, [P, PACK, P], U32, "kw%d" % e)
+            nc.vector.tensor_copy(
+                kw[e][:].rearrange("p t s -> p s t"), kw_pool[:].bitcast(U32).indirect(page_list(e))
             )
-            planes = sb([P, PACK, P], F32, "score_planes%d" % e)
-            nc.scalar.copy(planes[:], flat.rearrange("q (s t) -> q t s", t=PACK))
-            scores_t = bank("scores_t%d" % e, turned_tag)
-            for t in range(PACK):
-                nc.tensor.transpose(scores_t[:, t, :], planes[:, t, :], ident[:])
-            return scores_t
 
-        def weigh(e, scores_t):
-            pos = sb([P, PACK, NQ], F32, "pos%d" % e)
+        def score(e):
+            scores = bank("scores%d" % e, "scores%d" % e)
             for t in range(PACK):
-                nc.scalar.activation(pos[:, t, :], scores_t[:, t, :], ACT.Relu, bias=kb_col[e][:, t : t + 1])
+                nc.tensor.matmul_mx(
+                    scores[:, t, :], lhsT=kw[e][:, t, :].bitcast(FP8X4), lhsT_scale=ks[e][:, t, :],
+                    rhs=qw[:].bitcast(FP8X4), rhs_scale=qs[:], start=True, stop=True,
+                )
+            pos = sb([P, PACK, NQ], F32, "pos%d" % e, "w_planes0" if e == 2 else None)
+            for t in range(PACK):
+                nc.scalar.activation(pos[:, t, :], scores[:, t, :], ACT.Relu, bias=kb_col[e][:, t : t + 1])
             capped = sb([P, PACK, NQ], F32, "capped%d" % e)
             nc.scalar.activation(capped[:], pos[:], ACT.Tanh, scale=1.0 / CAP)
             p = sb([P, PACK, NQ], F32, "p%d" % e)
             nc.scalar.activation(p[:], capped[:], ACT.Square, scale=CAP)
-            return p
+            p_t.append(p)
 
-        scores_t0 = score(0, "bank0", "bank2")
-        gather_key_scales(2, "ks0_then_ks2")
-        scores_t1 = score(1, "bank1", "bank0")
-        gather_key_words(2, "ks1_then_kw2")
-        p_t = [weigh(0, scores_t0)]
-        p_t.append(weigh(1, scores_t1))
-        p_t.append(weigh(2, score(2, "bank0", "bank1")))
+        def token_scales(e, vs_row):
+            nc.vector.tensor_copy(vs_row, vs_pool[:].indirect(page_list(e)))
+            vs_col[e] = column("vs_col%d" % e, vs_row[BIAS_ROW:P, :])
 
-        vs_row = sb([P, N], F32, "vs_row", "keys_then_vs_row")
-        for e in range(PAGES):
-            nc.vector.tensor_copy(vs_row[:, page(e)], vs_pool[:].indirect(page_list(e)))
-        vs_banks = ("bank2", "bank0", "bank1")
-        vs_t = [turn("vs%d" % e, vs_row[:, page(e)], nc.vector.tensor_copy, vs_banks[e]) for e in range(PAGES)]
-        vw = sb([P, PAGES * DV], U32, "vw", "kb_then_vs_then_vw")
+        w = [sb([P, NQ * PACK], BF16, "w%d" % e) for e in range(PAGES)]
+
+        def weights_on_scalar(e):
+            planes = sb([P, PACK, NQ], BF16, "w_planes%d" % e)
+            for t in range(PACK):
+                nc.scalar.activation(planes[:, t, :], p_t[e][:, t, :], ACT.Copy, scale=vs_col[e][:, t : t + 1])
+            nc.scalar.copy(w[e][:].rearrange("s (q t) -> s q t", t=PACK), planes[:].rearrange("s t q -> s q t"))
+
+        deal(0, 2, key_scales(0, 2, 5120))
+        key_words(0, 14336)
+        key_words(1, 6144)
+        score(0)
+        score(1)
+        token_scales(0, at(14336 + 1024, [P, PAGE], F32, "vs_row0")[:])
+        weights_on_scalar(0)
+        last_row = key_scales(2, 1, 6144 - 448)
+        key_words(2, 6144 + 1984)
+        deal(2, 1, last_row)
+        score(2)
+        vs_rows = sb([P, 2, PAGE], F32, "vs_rows", "kw_pool_then_vs_rows")
+        token_scales(1, vs_rows[:, 0, :])
+        token_scales(2, vs_rows[:, 1, :])
+        vw = at(32768, [P, PAGES * DV], U32, "vw")
         nc.vector.tensor_copy(vw[:], vw_pool[:].bitcast(U32).indirect(value_list[:]))
-        vsc = sb([P, PAGES * DV], U8, "vsc", "kb_row_then_values")
+        vsc = at(0, [P, PAGES * DV], U8, "vsc")
         nc.vector.tensor_copy(vsc[:], vsc_pool[:].indirect(value_list[:]))
 
         total = psum.tile([P, P], F32, name="total")
-        acc = psum.tile([P, DV], F32, name="acc")
         nc.tensor.matmul(total[:], lhsT=ident[:], rhs=ident[:], is_transpose=True, start=True, stop=False)
         for e in range(PAGES):
             for t in range(PACK):
@@ -188,23 +197,19 @@ def tile_attend_pkv8q_rel2_cap_kb_kernel(
         parts = sb([P, P], F32, "parts")
         denom = sb([P, 1], F32, "denom")
         nc.scalar.activation(parts[:], total[:], ACT.Copy, accum_out=denom[:])
+        inv = sb([P, 1], F32, "inv")
+        nc.vector.reciprocal(inv[:], denom[:])
 
-        w = [sb([P, NQ * PACK], BF16, "w%d" % e) for e in range(PAGES)]
-        vs_col = sb([P, PACK], F32, "vs_col")
-        nc.scalar.copy(vs_col[:], vs_t[0][:, :, 0])
-        w_planes = sb([P, PACK, NQ], BF16, "w_planes")
-        for t in range(PACK):
-            nc.scalar.activation(w_planes[:, t, :], p_t[0][:, t, :], ACT.Copy, scale=vs_col[:, t : t + 1])
-        nc.scalar.copy(w[0][:].rearrange("s (q t) -> s q t", t=PACK), w_planes[:].rearrange("s t q -> s q t"))
         for e in range(1, PAGES):
             nc.vector.tensor_tensor(
                 w[e][:].rearrange("s (c i t) -> s c t i", i=PAIR, t=PACK),
                 p_t[e][:].rearrange("s t (c i) -> s c t i", i=PAIR),
-                vs_t[e][:].rearrange("s t (c i) -> s c t i", i=PAIR),
+                vs_col[e][:].unsqueeze(1).unsqueeze(3).to_broadcast([P, NQ // PAIR, PACK, PAIR]),
                 ALU.mult,
             )
 
-        order = (1, 0, 2)
+        acc = psum.tile([P, DV], F32, name="acc", tag="total")
+        order = (0, 1, 2)
         for e in order:
             w_codes = sb([P, NQ], U32, "w_codes%d" % e)
             w_scales = sb([P, NQ], U8, "w_scales%d" % e)
@@ -216,8 +221,6 @@ def tile_attend_pkv8q_rel2_cap_kb_kernel(
                 start=(e == order[0]), stop=(e == order[-1]),
             )
 
-        inv = sb([P, 1], F32, "inv")
-        nc.vector.reciprocal(inv[:], denom[:])
         y = sb([P, DV], F32, "y")
         nc.scalar.activation(y[:], acc[:], ACT.Copy, scale=inv[:])
         nc.sync.dma_start(out[0], y[:])

@@ -15,8 +15,7 @@ LIST_ROWS = 16
 BIAS_ROW = P - 1
 PAIR = 2
 
-KS_SPLIT = (640, 895)
-KB_SPLIT = (935, 1872)
+KB_SPLIT = (1169, 2336)
 
 FLOPS = 2 * NQ * N * D + 2 * NQ * N * DV
 BYTES = (T * D + T * DV + NQ * D) * 33 // 32 + 2 * 4 * T + 2 * P * (N + PAGES * DV) // LIST_ROWS + 4 * NQ * DV
@@ -64,10 +63,7 @@ def tile_attend_pkv8q_rel2_cap_kb_kernel(
         qs = sb([P, NQ], U8, "qs")
         ident = sb([P, P], F32, "ident")
 
-        ks_words = ks_pool[:].bitcast(I32)
-        nc.gpsimd.memset(ks_words[:, 0 : KS_SPLIT[0]], 0)
-        nc.vector.memset(ks_words[:, KS_SPLIT[0] : KS_SPLIT[1]], 0)
-        nc.vector.memset(ks_words[:, KS_SPLIT[1] : T // 4], 0)
+        nc.gpsimd.memset(ks_pool[:].bitcast(I32), 0)
         nc.vector.memset(kb_pool[0:BIAS_ROW, 0 : KB_SPLIT[0]], 0.0)
         nc.vector.memset(kb_pool[0:BIAS_ROW, KB_SPLIT[0] : KB_SPLIT[1]], 0.0)
         nc.gpsimd.memset(kb_pool[0:BIAS_ROW, KB_SPLIT[1] : T], 0.0)
@@ -146,7 +142,7 @@ def tile_attend_pkv8q_rel2_cap_kb_kernel(
                     scores[:, t, :], lhsT=kw[e][:, t, :].bitcast(FP8X4), lhsT_scale=ks[e][:, t, :],
                     rhs=qw[:].bitcast(FP8X4), rhs_scale=qs[:], start=True, stop=True,
                 )
-            pos = sb([P, PACK, NQ], F32, "pos%d" % e, "w_planes0" if e == 2 else None)
+            pos = sb([P, PACK, NQ], F32, "pos%d" % e, "w_planes1" if e == 2 else None)
             for t in range(PACK):
                 nc.scalar.activation(pos[:, t, :], scores[:, t, :], ACT.Relu, bias=kb_col[e][:, t : t + 1])
             capped = sb([P, PACK, NQ], F32, "capped%d" % e)
@@ -172,21 +168,23 @@ def tile_attend_pkv8q_rel2_cap_kb_kernel(
         key_words(1, 6144)
         score(0)
         score(1)
-        token_scales(0, at(14336 + 1024, [P, PAGE], F32, "vs_row0")[:])
+        vs_rows = at(14336 + 1024, [P, 2, PAGE], F32, "vs_rows")
+        token_scales(0, vs_rows[:, 0, :])
+        token_scales(1, vs_rows[:, 1, :])
         weights_on_scalar(0)
+        weights_on_scalar(1)
         last_row = key_scales(2, 1, 6144 - 448)
         key_words(2, 6144 + 1984)
         deal(2, 1, last_row)
         score(2)
-        vs_rows = sb([P, 2, PAGE], F32, "vs_rows", "kw_pool_then_vs_rows")
-        token_scales(1, vs_rows[:, 0, :])
-        token_scales(2, vs_rows[:, 1, :])
+        token_scales(2, sb([P, PAGE], F32, "vs_row2", "kw_pool_then_vs_rows")[:])
         vw = at(32768, [P, PAGES * DV], U32, "vw")
         nc.vector.tensor_copy(vw[:], vw_pool[:].bitcast(U32).indirect(value_list[:]))
         vsc = at(0, [P, PAGES * DV], U8, "vsc")
         nc.vector.tensor_copy(vsc[:], vsc_pool[:].indirect(value_list[:]))
 
         total = psum.tile([P, P], F32, name="total")
+        acc = psum.tile([P, DV], F32, name="acc")
         nc.tensor.matmul(total[:], lhsT=ident[:], rhs=ident[:], is_transpose=True, start=True, stop=False)
         for e in range(PAGES):
             for t in range(PACK):
@@ -200,7 +198,7 @@ def tile_attend_pkv8q_rel2_cap_kb_kernel(
         inv = sb([P, 1], F32, "inv")
         nc.vector.reciprocal(inv[:], denom[:])
 
-        for e in range(1, PAGES):
+        for e in range(PAGES - 1, PAGES):
             nc.vector.tensor_tensor(
                 w[e][:].rearrange("s (c i t) -> s c t i", i=PAIR, t=PACK),
                 p_t[e][:].rearrange("s t (c i) -> s c t i", i=PAIR),
@@ -208,7 +206,6 @@ def tile_attend_pkv8q_rel2_cap_kb_kernel(
                 ALU.mult,
             )
 
-        acc = psum.tile([P, DV], F32, name="acc", tag="total")
         order = (0, 1, 2)
         for e in order:
             w_codes = sb([P, NQ], U32, "w_codes%d" % e)

@@ -63,6 +63,10 @@ def tile_attend_pkv8q_rel2_cap_kb_kernel(
         qs = sb([P, NQ], U8, "qs")
         ident = sb([P, P], F32, "ident")
 
+        warm_in = sb([P, 1], F32, "warm_in")
+        warm_out = sb([P, 1], F32, "warm_out")
+        nc.gpsimd.memset(warm_in[:], 0.0)
+        nc.scalar.activation(warm_out[:], warm_in[:], ACT.Tanh)
         nc.gpsimd.memset(ks_pool[:].bitcast(I32), 0)
         nc.vector.memset(kb_pool[0:BIAS_ROW, 0 : KB_SPLIT[0]], 0.0)
         nc.vector.memset(kb_pool[0:BIAS_ROW, KB_SPLIT[0] : KB_SPLIT[1]], 0.0)
@@ -142,10 +146,10 @@ def tile_attend_pkv8q_rel2_cap_kb_kernel(
                     scores[:, t, :], lhsT=kw[e][:, t, :].bitcast(FP8X4), lhsT_scale=ks[e][:, t, :],
                     rhs=qw[:].bitcast(FP8X4), rhs_scale=qs[:], start=True, stop=True,
                 )
-            pos = sb([P, PACK, NQ], F32, "pos%d" % e, "w_planes1" if e == 2 else None)
+            pos = sb([P, PACK, NQ], F32, "pos%d" % e, "w_planes0" if e == 2 else None)
             for t in range(PACK):
                 nc.scalar.activation(pos[:, t, :], scores[:, t, :], ACT.Relu, bias=kb_col[e][:, t : t + 1])
-            capped = sb([P, PACK, NQ], F32, "capped%d" % e)
+            capped = at(55296 - 2048 * e, [P, PACK, NQ], F32, "capped%d" % e)
             nc.scalar.activation(capped[:], pos[:], ACT.Tanh, scale=1.0 / CAP)
             p = sb([P, PACK, NQ], F32, "p%d" % e)
             nc.scalar.activation(p[:], capped[:], ACT.Square, scale=CAP)
@@ -163,24 +167,25 @@ def tile_attend_pkv8q_rel2_cap_kb_kernel(
                 nc.scalar.activation(planes[:, t, :], p_t[e][:, t, :], ACT.Copy, scale=vs_col[e][:, t : t + 1])
             nc.scalar.copy(w[e][:].rearrange("s (q t) -> s q t", t=PACK), planes[:].rearrange("s t q -> s q t"))
 
-        deal(0, 2, key_scales(0, 2, 5120))
+        rows = [key_scales(e, 1, 57344 + 512 * e) for e in range(2)]
+        for e in range(2):
+            deal(e, 1, rows[e])
         key_words(0, 14336)
-        key_words(1, 6144)
+        key_words(1, 10240)
         score(0)
         score(1)
         vs_rows = at(14336 + 1024, [P, 2, PAGE], F32, "vs_rows")
         token_scales(0, vs_rows[:, 0, :])
         token_scales(1, vs_rows[:, 1, :])
         weights_on_scalar(0)
-        weights_on_scalar(1)
-        last_row = key_scales(2, 1, 6144 - 448)
-        key_words(2, 6144 + 1984)
+        last_row = key_scales(2, 1, 9792)
+        key_words(2, 12224)
         deal(2, 1, last_row)
         score(2)
         token_scales(2, sb([P, PAGE], F32, "vs_row2", "kw_pool_then_vs_rows")[:])
-        vw = at(32768, [P, PAGES * DV], U32, "vw")
+        vw = at(8320, [P, PAGES * DV], U32, "vw")
         nc.vector.tensor_copy(vw[:], vw_pool[:].bitcast(U32).indirect(value_list[:]))
-        vsc = at(0, [P, PAGES * DV], U8, "vsc")
+        vsc = at(9856, [P, PAGES * DV], U8, "vsc")
         nc.vector.tensor_copy(vsc[:], vsc_pool[:].indirect(value_list[:]))
 
         total = psum.tile([P, P], F32, name="total")
@@ -198,7 +203,7 @@ def tile_attend_pkv8q_rel2_cap_kb_kernel(
         inv = sb([P, 1], F32, "inv")
         nc.vector.reciprocal(inv[:], denom[:])
 
-        for e in range(PAGES - 1, PAGES):
+        for e in range(1, PAGES):
             nc.vector.tensor_tensor(
                 w[e][:].rearrange("s (c i t) -> s c t i", i=PAIR, t=PACK),
                 p_t[e][:].rearrange("s t (c i) -> s c t i", i=PAIR),
@@ -208,7 +213,7 @@ def tile_attend_pkv8q_rel2_cap_kb_kernel(
 
         order = (0, 1, 2)
         for e in order:
-            w_codes = sb([P, NQ], U32, "w_codes%d" % e)
+            w_codes = at(51200 + 512 * e, [P, NQ], U32, "w_codes%d" % e)
             w_scales = sb([P, NQ], U8, "w_scales%d" % e)
             nc.vector.quantize_mx(w_codes[:].bitcast(FP8X4), w_scales[:], w[e][:])
             cols = slice(e * DV, (e + 1) * DV)

@@ -13,6 +13,7 @@ PACK = 4
 QUADRANTS = 4
 LIST_ROWS = 16
 BIAS_ROW = P - 1
+HALF = 2
 PAIR = 2
 
 KB_SPLIT = (1169, 2336)
@@ -140,19 +141,24 @@ def tile_attend_pkv8q_rel2_cap_kb_kernel(
             )
 
         def score(e):
-            scores = bank("scores%d" % e, "scores%d" % e)
+            scores = [psum.tile([P, HALF, NQ], F32, name="scores%d_%d" % (e, h)) for h in range(PACK // HALF)]
             for t in range(PACK):
                 nc.tensor.matmul_mx(
-                    scores[:, t, :], lhsT=kw[e][:, t, :].bitcast(FP8X4), lhsT_scale=ks[e][:, t, :],
+                    scores[t // HALF][:, t % HALF, :], lhsT=kw[e][:, t, :].bitcast(FP8X4), lhsT_scale=ks[e][:, t, :],
                     rhs=qw[:].bitcast(FP8X4), rhs_scale=qs[:], start=True, stop=True,
                 )
-            pos = sb([P, PACK, NQ], F32, "pos%d" % e, "w_planes0" if e == 2 else None)
+            pos = sb([P, PACK, NQ], F32, "pos%d" % e, "vs_col0" if e == 2 else None)
             for t in range(PACK):
-                nc.scalar.activation(pos[:, t, :], scores[:, t, :], ACT.Relu, bias=kb_col[e][:, t : t + 1])
+                nc.scalar.activation(
+                    pos[:, t, :], scores[t // HALF][:, t % HALF, :], ACT.Relu, bias=kb_col[e][:, t : t + 1]
+                )
             capped = at(55296 - 2048 * e, [P, PACK, NQ], F32, "capped%d" % e)
-            nc.scalar.activation(capped[:], pos[:], ACT.Tanh, scale=1.0 / CAP)
             p = sb([P, PACK, NQ], F32, "p%d" % e)
-            nc.scalar.activation(p[:], capped[:], ACT.Square, scale=CAP)
+            halves = [slice(h, h + HALF) for h in range(0, PACK, HALF)]
+            for h in halves:
+                nc.scalar.activation(capped[:, h, :], pos[:, h, :], ACT.Tanh, scale=1.0 / CAP)
+            for h in halves:
+                nc.scalar.activation(p[:, h, :], capped[:, h, :], ACT.Square, scale=CAP)
             p_t.append(p)
 
         def token_scales(e, vs_row):
@@ -171,21 +177,21 @@ def tile_attend_pkv8q_rel2_cap_kb_kernel(
         for e in range(2):
             deal(e, 1, rows[e])
         key_words(0, 14336)
-        key_words(1, 10240)
         score(0)
+        token_scales(0, sb([P, PAGE], F32, "vs_row0")[:])
+        key_words(1, 10240)
         score(1)
-        vs_rows = at(14336 + 1024, [P, 2, PAGE], F32, "vs_rows")
-        token_scales(0, vs_rows[:, 0, :])
-        token_scales(1, vs_rows[:, 1, :])
         weights_on_scalar(0)
-        last_row = key_scales(2, 1, 9792)
+        last_row = key_scales(2, 1, 16320)
         key_words(2, 12224)
         deal(2, 1, last_row)
         score(2)
-        token_scales(2, sb([P, PAGE], F32, "vs_row2", "kw_pool_then_vs_rows")[:])
-        vw = at(8320, [P, PAGES * DV], U32, "vw")
+        vs_rows = sb([P, 2, PAGE], F32, "vs_rows", "kw_pool_then_vs_rows")
+        token_scales(1, vs_rows[:, 0, :])
+        token_scales(2, vs_rows[:, 1, :])
+        vw = at(16768, [P, PAGES * DV], U32, "vw")
         nc.vector.tensor_copy(vw[:], vw_pool[:].bitcast(U32).indirect(value_list[:]))
-        vsc = at(9856, [P, PAGES * DV], U8, "vsc")
+        vsc = at(16384, [P, PAGES * DV], U8, "vsc")
         nc.vector.tensor_copy(vsc[:], vsc_pool[:].indirect(value_list[:]))
 
         total = psum.tile([P, P], F32, name="total")

@@ -165,6 +165,15 @@ def tile_attend_pkv8q_rel2_cap_kb_kernel(
             nc.vector.tensor_copy(vs_row, vs_pool[:].indirect(page_list(e)))
             vs_col[e] = column("vs_col%d" % e, vs_row[BIAS_ROW:P, :])
 
+        def token_scales_turned(e, planes):
+            nc.vector.tensor_copy(
+                planes.bitcast(U32).rearrange("p t s -> p s t"), vs_pool[:].bitcast(U32).indirect(page_list(e))
+            )
+            turned = psum.tile([P, PACK, P], F32, name="vs_t%d" % e, tag="scores0_%d" % (e - 1))
+            for t in range(PACK):
+                nc.tensor.transpose(turned[:, t, :], planes[:, t, :], ident[:])
+            return turned[:, :, BIAS_ROW]
+
         w = [sb([P, NQ * PACK], BF16, "w%d" % e) for e in range(PAGES)]
 
         def weights_on_scalar(e):
@@ -186,9 +195,9 @@ def tile_attend_pkv8q_rel2_cap_kb_kernel(
         key_words(2, 12224)
         deal(2, 1, last_row)
         score(2)
-        vs_rows = sb([P, 2, PAGE], F32, "vs_rows", "kw_pool_then_vs_rows")
-        token_scales(1, vs_rows[:, 0, :])
-        token_scales(2, vs_rows[:, 1, :])
+        vs_rows = sb([P, 2, PACK, P], F32, "vs_rows", "kw_pool_then_vs_rows")
+        for e in range(1, PAGES):
+            vs_col[e] = token_scales_turned(e, vs_rows[:, e - 1, :, :])
         vw = at(16768, [P, PAGES * DV], U32, "vw")
         nc.vector.tensor_copy(vw[:], vw_pool[:].bitcast(U32).indirect(value_list[:]))
         vsc = at(16384, [P, PAGES * DV], U8, "vsc")
@@ -213,7 +222,7 @@ def tile_attend_pkv8q_rel2_cap_kb_kernel(
             nc.vector.tensor_tensor(
                 w[e][:].rearrange("s (c i t) -> s c t i", i=PAIR, t=PACK),
                 p_t[e][:].rearrange("s t (c i) -> s c t i", i=PAIR),
-                vs_col[e][:].unsqueeze(1).unsqueeze(3).to_broadcast([P, NQ // PAIR, PACK, PAIR]),
+                vs_col[e].unsqueeze(1).unsqueeze(3).to_broadcast([P, NQ // PAIR, PACK, PAIR]),
                 ALU.mult,
             )
 

@@ -64,10 +64,6 @@ def tile_attend_pkv8q_rel2_cap_kb_kernel(
         qs = sb([P, NQ], U8, "qs")
         ident = sb([P, P], F32, "ident")
 
-        warm_in = sb([P, 1], F32, "warm_in")
-        warm_out = sb([P, 1], F32, "warm_out")
-        nc.gpsimd.memset(warm_in[:], 0.0)
-        nc.scalar.activation(warm_out[:], warm_in[:], ACT.Tanh)
         nc.gpsimd.memset(ks_pool[:].bitcast(I32), 0)
         nc.vector.memset(kb_pool[0:BIAS_ROW, 0 : KB_SPLIT[0]], 0.0)
         nc.vector.memset(kb_pool[0:BIAS_ROW, KB_SPLIT[0] : KB_SPLIT[1]], 0.0)

@@ -1,7 +1,6 @@
 from contextlib import ExitStack
 
 import concourse.mybir as mybir
-from concourse.masks import make_identity
 
 N, T, D, DV, NQ = 1536, 4096, 512, 128, 128
 PAGE = 512
@@ -16,7 +15,8 @@ BIAS_ROW = P - 1
 HALF = 2
 PAIR = 2
 
-KB_SPLIT = (1169, 2336)
+KB_SPLIT = (1201, 2400)
+VS_SPLIT = (401, 800)
 
 FLOPS = 2 * NQ * N * D + 2 * NQ * N * DV
 BYTES = (T * D + T * DV + NQ * D) * 33 // 32 + 2 * 4 * T + 2 * P * (N + PAGES * DV) // LIST_ROWS + 4 * NQ * DV
@@ -48,58 +48,59 @@ def tile_attend_pkv8q_rel2_cap_kb_kernel(
         def at(offset, shape, dtype, name):
             return placed.tile(shape, dtype, name=name, align_bytes=64, offset=offset)
 
-        def bank(name, tag):
-            return psum.tile([P, PACK, P], F32, name=name, tag=tag)
-
         def scale_rows(plane, g):
             return plane[32 * g : 32 * g + 4, :].bitcast(I32)
 
         key_list = lists.tile([P, N // LIST_ROWS], U16, name="key_list")
         value_list = lists.tile([P, PAGES * DV // LIST_ROWS], U16, name="value_list")
-        kw_pool = sb([P, T], I32, "kw_pool", "kw_pool_then_vs_rows")
+        steps = at(32768 - 256, [P, P], F32, "steps")
+        squares = at(49152, [P, P], F32, "squares")
+        kw_pool = at(32768, [P, T], I32, "kw_pool")
         ks_pool = sb([P, T], U8, "ks_pool")
         kb_pool = at(0, [P, T], F32, "kb_pool")
-        vs_pool = at(32768, [P, T], F32, "vs_pool")
-        qw = sb([P, NQ], I32, "qw")
+        vs_pool = at(16384, [P, T], F32, "vs_pool")
+        qw = at(49152, [P, NQ], I32, "qw")
         qs = sb([P, NQ], U8, "qs")
         ident = sb([P, P], F32, "ident")
 
+        nc.gpsimd.iota(steps[:], [[1, P]], base=0, channel_multiplier=-1, allow_small_or_imprecise_dtypes=True)
         nc.gpsimd.memset(ks_pool[:].bitcast(I32), 0)
+        nc.gpsimd.tensor_tensor(squares[:], steps[:], steps[:], ALU.mult)
+        nc.scalar.activation(ident[:], squares[:], ACT.Relu, scale=-1.0, bias=1.0)
+        nc.gpsimd.memset(qs[:].bitcast(I32), 0)
         nc.vector.memset(kb_pool[0:BIAS_ROW, 0 : KB_SPLIT[0]], 0.0)
         nc.vector.memset(kb_pool[0:BIAS_ROW, KB_SPLIT[0] : KB_SPLIT[1]], 0.0)
         nc.gpsimd.memset(kb_pool[0:BIAS_ROW, KB_SPLIT[1] : T], 0.0)
-        nc.gpsimd.memset(qs[:].bitcast(I32), 0)
-        nc.gpsimd.memset(ident[:], 0.0)
-        nc.gpsimd.memset(vs_pool[0:BIAS_ROW, :], 0.0)
-        make_identity(nc, ident[:], nomemset=True)
+        nc.vector.memset(vs_pool[0:BIAS_ROW, 0 : VS_SPLIT[0]], 0.0)
+        nc.vector.memset(vs_pool[0:BIAS_ROW, VS_SPLIT[0] : VS_SPLIT[1]], 0.0)
+        nc.gpsimd.memset(vs_pool[0:BIAS_ROW, VS_SPLIT[1] : T], 0.0)
 
         nc.sync.dma_start(key_list[:], offs)
         nc.sync.dma_start(kb_pool[BIAS_ROW:P, :], kb[0:1, :])
         nc.sync.dma_start(value_list[:], voffs)
-        nc.sync.dma_start(qw[:], q_words[0, 0].rearrange("p q r -> p (q r)").bitcast(I32))
+        for g in range(QUADRANTS):
+            nc.sync.dma_start(scale_rows(ks_pool, g), k_scales[0, 4 * g : 4 * g + 4, :].bitcast(I32))
         nc.sync.dma_start(kw_pool[:], k_words[0].rearrange("p t r -> p (t r)").bitcast(I32))
-        nc.sync.dma_start(vs_pool[BIAS_ROW:P, :], vs[0:1, :])
+        nc.scalar.dma_start(vs_pool[BIAS_ROW:P, :], vs[0:1, :])
+        nc.sync.dma_start(qw[:], q_words[0, 0].rearrange("p q r -> p (q r)").bitcast(I32))
         for g in range(QUADRANTS):
-            nc.scalar.dma_start(scale_rows(ks_pool, g), k_scales[0, 4 * g : 4 * g + 4, :].bitcast(I32))
-        for g in range(QUADRANTS):
-            queue = nc.scalar if g < 2 else nc.sync
-            queue.dma_start(scale_rows(qs, g), q_scales[0, 0, 4 * g : 4 * g + 4, :].bitcast(I32))
+            nc.sync.dma_start(scale_rows(qs, g), q_scales[0, 0, 4 * g : 4 * g + 4, :].bitcast(I32))
 
         def page_list(e):
             cols = PAGE // LIST_ROWS
             return key_list[:, e * cols : (e + 1) * cols]
 
-        def page(e):
-            return slice(e * PAGE, (e + 1) * PAGE)
+        def columns(name, pool):
+            cols = []
+            for e in range(PAGES):
+                row = sb([P, PAGE], F32, "%s_row%d" % (name, e))
+                nc.scalar.activation(row[:], pool[:].indirect(page_list(e)), ACT.Copy)
+                col = sb([P, PACK], F32, "%s_col%d" % (name, e))
+                nc.sync.dma_start(col[:], row[BIAS_ROW:P, :])
+                cols.append(col)
+            return cols
 
-        def column(name, row):
-            col = sb([P, PACK], F32, name)
-            nc.sync.dma_start(col[:], row)
-            return col
-
-        kb_row = sb([P, N], F32, "kb_row")
-        nc.vector.tensor_copy(kb_row[:], kb_pool[:].indirect(key_list[:]))
-        kb_col = [column("kb_col%d" % e, kb_row[BIAS_ROW:P, page(e)]) for e in range(PAGES)]
+        kb_col = columns("kb", kb_pool)
 
         vw_pool = at(0, [P, POOL_PAGES * DV], I32, "vw_pool")
         nc.sync.dma_start(
@@ -113,90 +114,40 @@ def tile_attend_pkv8q_rel2_cap_kb_kernel(
                 scale_rows(vsc_pool, g).rearrange("p (u e) -> p u e", u=POOL_PAGES),
                 v_scales[:, 4 * g : 4 * g + 4, :].rearrange("u f e -> f u e").bitcast(I32),
             )
+        vs_col = columns("vs", vs_pool)
 
-        vs_col, p_t = {}, []
+        ks_row = sb([P, N], U8, "ks_row")
+        nc.vector.tensor_copy(ks_row[:], ks_pool[:].indirect(key_list[:]))
+        ks = sb([P, PAGES, PACK, P], U8, "ks")
+        nc.vector.tensor_copy(ks[:], ks_row[:].rearrange("p (e s t) -> p e t s", e=PAGES, t=PACK))
 
-        ks, kw = {}, {}
-
-        def key_scales(first, count, row_at):
-            cols = PAGE // LIST_ROWS
-            row = at(row_at, [P, count * PAGE], U8, "ks_row%d" % first)
-            nc.vector.tensor_copy(row[:], ks_pool[:].indirect(key_list[:, first * cols : (first + count) * cols]))
-            return row
-
-        def deal(first, count, row):
-            dealt = sb([P, count, PACK, P], U8, "ks%d" % first)
-            nc.vector.tensor_copy(dealt[:], row[:].rearrange("p (e s t) -> p e t s", e=count, t=PACK))
-            for e in range(count):
-                ks[first + e] = dealt[:, e, :, :]
-
-        def key_words(e, kw_at):
-            kw[e] = at(kw_at, [P, PACK, P], U32, "kw%d" % e)
-            nc.vector.tensor_copy(
-                kw[e][:].rearrange("p t s -> p s t"), kw_pool[:].bitcast(U32).indirect(page_list(e))
-            )
-
-        def score(e):
+        halves = [slice(h, h + HALF) for h in range(0, PACK, HALF)]
+        p_t = []
+        for e in range(PAGES):
+            kw = sb([P, PACK, P], U32, "kw%d" % e)
+            nc.vector.tensor_copy(kw[:].rearrange("p t s -> p s t"), kw_pool[:].bitcast(U32).indirect(page_list(e)))
             scores = [psum.tile([P, HALF, NQ], F32, name="scores%d_%d" % (e, h)) for h in range(PACK // HALF)]
             for t in range(PACK):
                 nc.tensor.matmul_mx(
-                    scores[t // HALF][:, t % HALF, :], lhsT=kw[e][:, t, :].bitcast(FP8X4), lhsT_scale=ks[e][:, t, :],
+                    scores[t // HALF][:, t % HALF, :], lhsT=kw[:, t, :].bitcast(FP8X4), lhsT_scale=ks[:, e, t, :],
                     rhs=qw[:].bitcast(FP8X4), rhs_scale=qs[:], start=True, stop=True,
                 )
-            pos = sb([P, PACK, NQ], F32, "pos%d" % e, "vs_col0" if e == 2 else None)
+            pos = sb([P, PACK, NQ], F32, "pos%d" % e, "pos")
             for t in range(PACK):
                 nc.scalar.activation(
                     pos[:, t, :], scores[t // HALF][:, t % HALF, :], ACT.Relu, bias=kb_col[e][:, t : t + 1]
                 )
-            capped = at(55296 - 2048 * e, [P, PACK, NQ], F32, "capped%d" % e)
+            capped = sb([P, PACK, NQ], F32, "capped%d" % e)
             p = sb([P, PACK, NQ], F32, "p%d" % e)
-            halves = [slice(h, h + HALF) for h in range(0, PACK, HALF)]
             for h in halves:
                 nc.scalar.activation(capped[:, h, :], pos[:, h, :], ACT.Tanh, scale=1.0 / CAP)
             for h in halves:
                 nc.scalar.activation(p[:, h, :], capped[:, h, :], ACT.Square, scale=CAP)
             p_t.append(p)
 
-        def token_scales(e, vs_row):
-            nc.vector.tensor_copy(vs_row, vs_pool[:].indirect(page_list(e)))
-            vs_col[e] = column("vs_col%d" % e, vs_row[BIAS_ROW:P, :])
-
-        def token_scales_turned(e, planes):
-            nc.vector.tensor_copy(
-                planes.bitcast(U32).rearrange("p t s -> p s t"), vs_pool[:].bitcast(U32).indirect(page_list(e))
-            )
-            turned = psum.tile([P, PACK, P], F32, name="vs_t%d" % e, tag="scores0_%d" % (e - 1))
-            for t in range(PACK):
-                nc.tensor.transpose(turned[:, t, :], planes[:, t, :], ident[:])
-            return turned[:, :, BIAS_ROW]
-
-        w = [sb([P, NQ * PACK], BF16, "w%d" % e) for e in range(PAGES)]
-
-        def weights_on_scalar(e):
-            planes = sb([P, PACK, NQ], BF16, "w_planes%d" % e)
-            for t in range(PACK):
-                nc.scalar.activation(planes[:, t, :], p_t[e][:, t, :], ACT.Copy, scale=vs_col[e][:, t : t + 1])
-            nc.scalar.copy(w[e][:].rearrange("s (q t) -> s q t", t=PACK), planes[:].rearrange("s t q -> s q t"))
-
-        rows = [key_scales(e, 1, 57344 + 512 * e) for e in range(2)]
-        for e in range(2):
-            deal(e, 1, rows[e])
-        key_words(0, 14336)
-        score(0)
-        token_scales(0, sb([P, PAGE], F32, "vs_row0")[:])
-        key_words(1, 10240)
-        score(1)
-        weights_on_scalar(0)
-        last_row = key_scales(2, 1, 16320)
-        key_words(2, 12224)
-        deal(2, 1, last_row)
-        score(2)
-        vs_rows = sb([P, 2, PACK, P], F32, "vs_rows", "kw_pool_then_vs_rows")
-        for e in range(1, PAGES):
-            vs_col[e] = token_scales_turned(e, vs_rows[:, e - 1, :, :])
-        vw = at(16768, [P, PAGES * DV], U32, "vw")
+        vw = sb([P, PAGES * DV], U32, "vw")
         nc.vector.tensor_copy(vw[:], vw_pool[:].bitcast(U32).indirect(value_list[:]))
-        vsc = at(16384, [P, PAGES * DV], U8, "vsc")
+        vsc = sb([P, PAGES * DV], U8, "vsc")
         nc.vector.tensor_copy(vsc[:], vsc_pool[:].indirect(value_list[:]))
 
         total = psum.tile([P, P], F32, name="total")
@@ -211,27 +162,26 @@ def tile_attend_pkv8q_rel2_cap_kb_kernel(
         parts = sb([P, P], F32, "parts")
         denom = sb([P, 1], F32, "denom")
         nc.scalar.activation(parts[:], total[:], ACT.Copy, accum_out=denom[:])
-        inv = sb([P, 1], F32, "inv")
-        nc.vector.reciprocal(inv[:], denom[:])
 
-        for e in range(1, PAGES):
+        w = [sb([P, NQ * PACK], BF16, "w%d" % e) for e in range(PAGES)]
+        for e in range(PAGES):
             nc.vector.tensor_tensor(
                 w[e][:].rearrange("s (c i t) -> s c t i", i=PAIR, t=PACK),
                 p_t[e][:].rearrange("s t (c i) -> s c t i", i=PAIR),
-                vs_col[e].unsqueeze(1).unsqueeze(3).to_broadcast([P, NQ // PAIR, PACK, PAIR]),
+                vs_col[e][:].unsqueeze(1).unsqueeze(3).to_broadcast([P, NQ // PAIR, PACK, PAIR]),
                 ALU.mult,
             )
-
-        order = (0, 1, 2)
-        for e in order:
-            w_codes = at(51200 + 512 * e, [P, NQ], U32, "w_codes%d" % e)
+        inv = sb([P, 1], F32, "inv")
+        nc.vector.reciprocal(inv[:], denom[:])
+        for e in range(PAGES):
+            w_codes = sb([P, NQ], U32, "w_codes%d" % e)
             w_scales = sb([P, NQ], U8, "w_scales%d" % e)
             nc.vector.quantize_mx(w_codes[:].bitcast(FP8X4), w_scales[:], w[e][:])
             cols = slice(e * DV, (e + 1) * DV)
             nc.tensor.matmul_mx(
                 acc[:], lhsT=w_codes[:].bitcast(FP8X4), lhsT_scale=w_scales[:],
                 rhs=vw[:, cols].bitcast(FP8X4), rhs_scale=vsc[:, cols],
-                start=(e == order[0]), stop=(e == order[-1]),
+                start=(e == 0), stop=(e == PAGES - 1),
             )
 
         y = sb([P, DV], F32, "y")

@@ -53,21 +53,21 @@ def tile_attend_pkv8q_rel2_cap_kb_kernel(
 
         key_list = lists.tile([P, N // LIST_ROWS], U16, name="key_list")
         value_list = lists.tile([P, PAGES * DV // LIST_ROWS], U16, name="value_list")
-        steps = at(32768 - 256, [P, P], F32, "steps")
-        squares = at(49152, [P, P], F32, "squares")
-        kw_pool = at(32768, [P, T], I32, "kw_pool")
+        steps = sb([P, P], F32, "steps")
+        distance = sb([P, P], F32, "distance")
+        kw_pool = sb([P, T], I32, "kw_pool")
         ks_pool = sb([P, T], U8, "ks_pool")
         kb_pool = at(0, [P, T], F32, "kb_pool")
         vs_pool = at(16384, [P, T], F32, "vs_pool")
-        qw = at(49152, [P, NQ], I32, "qw")
+        qw = sb([P, NQ], I32, "qw")
         qs = sb([P, NQ], U8, "qs")
         ident = sb([P, P], F32, "ident")
 
+        nc.gpsimd.memset(qs[:].bitcast(I32), 0)
         nc.gpsimd.iota(steps[:], [[1, P]], base=0, channel_multiplier=-1, allow_small_or_imprecise_dtypes=True)
         nc.gpsimd.memset(ks_pool[:].bitcast(I32), 0)
-        nc.gpsimd.tensor_tensor(squares[:], steps[:], steps[:], ALU.mult)
-        nc.scalar.activation(ident[:], squares[:], ACT.Relu, scale=-1.0, bias=1.0)
-        nc.gpsimd.memset(qs[:].bitcast(I32), 0)
+        nc.scalar.activation(distance[:], steps[:], ACT.Abs)
+        nc.scalar.activation(ident[:], distance[:], ACT.Relu, scale=-1.0, bias=1.0)
         nc.vector.memset(kb_pool[0:BIAS_ROW, 0 : KB_SPLIT[0]], 0.0)
         nc.vector.memset(kb_pool[0:BIAS_ROW, KB_SPLIT[0] : KB_SPLIT[1]], 0.0)
         nc.gpsimd.memset(kb_pool[0:BIAS_ROW, KB_SPLIT[1] : T], 0.0)
@@ -78,29 +78,30 @@ def tile_attend_pkv8q_rel2_cap_kb_kernel(
         nc.sync.dma_start(key_list[:], offs)
         nc.sync.dma_start(kb_pool[BIAS_ROW:P, :], kb[0:1, :])
         nc.sync.dma_start(value_list[:], voffs)
-        for g in range(QUADRANTS):
-            nc.sync.dma_start(scale_rows(ks_pool, g), k_scales[0, 4 * g : 4 * g + 4, :].bitcast(I32))
-        nc.sync.dma_start(kw_pool[:], k_words[0].rearrange("p t r -> p (t r)").bitcast(I32))
-        nc.scalar.dma_start(vs_pool[BIAS_ROW:P, :], vs[0:1, :])
+        nc.sync.dma_start(vs_pool[BIAS_ROW:P, :], vs[0:1, :])
         nc.sync.dma_start(qw[:], q_words[0, 0].rearrange("p q r -> p (q r)").bitcast(I32))
         for g in range(QUADRANTS):
+            if g == 2:
+                nc.sync.dma_start(kw_pool[:], k_words[0].rearrange("p t r -> p (t r)").bitcast(I32))
             nc.sync.dma_start(scale_rows(qs, g), q_scales[0, 0, 4 * g : 4 * g + 4, :].bitcast(I32))
+        for g in range(QUADRANTS):
+            nc.scalar.dma_start(scale_rows(ks_pool, g), k_scales[0, 4 * g : 4 * g + 4, :].bitcast(I32))
 
         def page_list(e):
             cols = PAGE // LIST_ROWS
             return key_list[:, e * cols : (e + 1) * cols]
 
-        def columns(name, pool):
+        def columns(name, pool, factor):
             cols = []
             for e in range(PAGES):
                 row = sb([P, PAGE], F32, "%s_row%d" % (name, e))
-                nc.scalar.activation(row[:], pool[:].indirect(page_list(e)), ACT.Copy)
+                nc.scalar.activation(row[:], pool[:].indirect(page_list(e)), ACT.Copy, scale=factor)
                 col = sb([P, PACK], F32, "%s_col%d" % (name, e))
                 nc.sync.dma_start(col[:], row[BIAS_ROW:P, :])
                 cols.append(col)
             return cols
 
-        kb_col = columns("kb", kb_pool)
+        kb_col = columns("kb", kb_pool, 1.0 / CAP)
 
         vw_pool = at(0, [P, POOL_PAGES * DV], I32, "vw_pool")
         nc.sync.dma_start(
@@ -114,66 +115,78 @@ def tile_attend_pkv8q_rel2_cap_kb_kernel(
                 scale_rows(vsc_pool, g).rearrange("p (u e) -> p u e", u=POOL_PAGES),
                 v_scales[:, 4 * g : 4 * g + 4, :].rearrange("u f e -> f u e").bitcast(I32),
             )
-        vs_col = columns("vs", vs_pool)
+        vs_col = columns("vs", vs_pool, CAP * CAP)
 
-        ks_row = sb([P, N], U8, "ks_row")
-        nc.vector.tensor_copy(ks_row[:], ks_pool[:].indirect(key_list[:]))
-        ks = sb([P, PAGES, PACK, P], U8, "ks")
-        nc.vector.tensor_copy(ks[:], ks_row[:].rearrange("p (e s t) -> p e t s", e=PAGES, t=PACK))
+        ks_row = at(33792, [P, T], U8, "ks_row")[:, 0:N]
+        nc.vector.tensor_copy(ks_row, ks_pool[:].indirect(key_list[:]))
+        ks = sb([P, PACK, PAGES, P], U8, "ks")
+        nc.vector.tensor_copy(ks[:], ks_row.rearrange("p (e s t) -> p t e s", e=PAGES, t=PACK))
 
         halves = [slice(h, h + HALF) for h in range(0, PACK, HALF)]
-        p_t = []
+        capped = []
+        p_t = [sb([P, PACK, NQ], F32, "p%d" % e) for e in range(PAGES)]
+
+        def square_on_scalar(e):
+            pos = sb([P, PACK, NQ], F32, "pos0") if e == 0 else at(32768 + 4096, [P, PACK, NQ], F32, "pos1")
+            for h in halves:
+                nc.scalar.activation(pos[:, h, :], capped[e][:, h, :], ACT.Relu)
+            for h in halves:
+                nc.scalar.activation(p_t[e][:, h, :], pos[:, h, :], ACT.Square)
+
         for e in range(PAGES):
-            kw = sb([P, PACK, P], U32, "kw%d" % e)
+            kw = at(32768 + 2048 * e, [P, PACK, P], U32, "kw%d" % e)
             nc.vector.tensor_copy(kw[:].rearrange("p t s -> p s t"), kw_pool[:].bitcast(U32).indirect(page_list(e)))
             scores = [psum.tile([P, HALF, NQ], F32, name="scores%d_%d" % (e, h)) for h in range(PACK // HALF)]
             for t in range(PACK):
                 nc.tensor.matmul_mx(
-                    scores[t // HALF][:, t % HALF, :], lhsT=kw[:, t, :].bitcast(FP8X4), lhsT_scale=ks[:, e, t, :],
+                    scores[t // HALF][:, t % HALF, :], lhsT=kw[:, t, :].bitcast(FP8X4), lhsT_scale=ks[:, t, e, :],
                     rhs=qw[:].bitcast(FP8X4), rhs_scale=qs[:], start=True, stop=True,
                 )
-            pos = sb([P, PACK, NQ], F32, "pos%d" % e, "pos")
+            capped.append(at(16384 + 2048 * e, [P, PACK, NQ], F32, "capped%d" % e))
             for t in range(PACK):
                 nc.scalar.activation(
-                    pos[:, t, :], scores[t // HALF][:, t % HALF, :], ACT.Relu, bias=kb_col[e][:, t : t + 1]
+                    capped[e][:, t, :], scores[t // HALF][:, t % HALF, :], ACT.Tanh,
+                    scale=1.0 / CAP, bias=kb_col[e][:, t : t + 1],
                 )
-            capped = sb([P, PACK, NQ], F32, "capped%d" % e)
-            p = sb([P, PACK, NQ], F32, "p%d" % e)
-            for h in halves:
-                nc.scalar.activation(capped[:, h, :], pos[:, h, :], ACT.Tanh, scale=1.0 / CAP)
-            for h in halves:
-                nc.scalar.activation(p[:, h, :], capped[:, h, :], ACT.Square, scale=CAP)
-            p_t.append(p)
+            if e == 0:
+                square_on_scalar(0)
+        square_on_scalar(1)
 
-        vw = sb([P, PAGES * DV], U32, "vw")
+        vw = at(32768, [P, PAGES * DV], U32, "vw")
         nc.vector.tensor_copy(vw[:], vw_pool[:].bitcast(U32).indirect(value_list[:]))
-        vsc = sb([P, PAGES * DV], U8, "vsc")
+        vsc = at(32768 + 1536, [P, PAGES * DV], U8, "vsc")
         nc.vector.tensor_copy(vsc[:], vsc_pool[:].indirect(value_list[:]))
 
-        total = psum.tile([P, P], F32, name="total")
-        acc = psum.tile([P, DV], F32, name="acc")
-        nc.tensor.matmul(total[:], lhsT=ident[:], rhs=ident[:], is_transpose=True, start=True, stop=False)
-        for e in range(PAGES):
-            for t in range(PACK):
-                nc.tensor.matmul(
-                    total[:], lhsT=p_t[e][:, t, :], rhs=ident[:], is_transpose=True,
-                    start=False, stop=(e == PAGES - 1 and t == PACK - 1),
-                )
-        parts = sb([P, P], F32, "parts")
-        denom = sb([P, 1], F32, "denom")
-        nc.scalar.activation(parts[:], total[:], ACT.Copy, accum_out=denom[:])
-
+        order = (0, 2, 1)
         w = [sb([P, NQ * PACK], BF16, "w%d" % e) for e in range(PAGES)]
-        for e in range(PAGES):
+
+        def weights(e):
             nc.vector.tensor_tensor(
                 w[e][:].rearrange("s (c i t) -> s c t i", i=PAIR, t=PACK),
                 p_t[e][:].rearrange("s t (c i) -> s c t i", i=PAIR),
                 vs_col[e][:].unsqueeze(1).unsqueeze(3).to_broadcast([P, NQ // PAIR, PACK, PAIR]),
                 ALU.mult,
             )
+
+        weights(0)
+        nc.vector.scalar_tensor_tensor(p_t[2][:], capped[2][:], 0.0, capped[2][:], ALU.max, ALU.mult)
+        weights(2)
+        weights(1)
+
+        total = psum.tile([P, P], F32, name="total")
+        acc = psum.tile([P, DV], F32, name="acc")
+        for e in order:
+            for t in range(PACK):
+                nc.tensor.matmul(
+                    total[:], lhsT=p_t[e][:, t, :], rhs=ident[:], is_transpose=True,
+                    start=(e == order[0] and t == 0), stop=(e == order[-1] and t == PACK - 1),
+                )
+        parts = sb([P, P], F32, "parts")
+        denom = sb([P, 1], F32, "denom")
+        nc.scalar.activation(parts[:], total[:], ACT.Copy, scale=CAP * CAP, bias=1.0 / P, accum_out=denom[:])
         inv = sb([P, 1], F32, "inv")
         nc.vector.reciprocal(inv[:], denom[:])
-        for e in range(PAGES):
+        for e in order:
             w_codes = sb([P, NQ], U32, "w_codes%d" % e)
             w_scales = sb([P, NQ], U8, "w_scales%d" % e)
             nc.vector.quantize_mx(w_codes[:].bitcast(FP8X4), w_scales[:], w[e][:])
@@ -181,7 +194,7 @@ def tile_attend_pkv8q_rel2_cap_kb_kernel(
             nc.tensor.matmul_mx(
                 acc[:], lhsT=w_codes[:].bitcast(FP8X4), lhsT_scale=w_scales[:],
                 rhs=vw[:, cols].bitcast(FP8X4), rhs_scale=vsc[:, cols],
-                start=(e == 0), stop=(e == PAGES - 1),
+                start=(e == order[0]), stop=(e == order[-1]),
             )
 
         y = sb([P, DV], F32, "y")

@@ -1,6 +1,7 @@
 from contextlib import ExitStack
 
 import concourse.mybir as mybir
+from concourse.masks import make_identity
 
 N, T, D, DV, NQ = 1536, 4096, 512, 128, 128
 PAGE = 512
@@ -15,8 +16,9 @@ BIAS_ROW = P - 1
 HALF = 2
 PAIR = 2
 
-KB_SPLIT = (1201, 2400)
-VS_SPLIT = (401, 800)
+KW_FIRST = 1024
+KB_SPLIT = (1161, 2320)
+VS_SPLIT = (545, 1088)
 
 FLOPS = 2 * NQ * N * D + 2 * NQ * N * DV
 BYTES = (T * D + T * DV + NQ * D) * 33 // 32 + 2 * 4 * T + 2 * P * (N + PAGES * DV) // LIST_ROWS + 4 * NQ * DV
@@ -53,24 +55,23 @@ def tile_attend_pkv8q_rel2_cap_kb_kernel(
 
         key_list = lists.tile([P, N // LIST_ROWS], U16, name="key_list")
         value_list = lists.tile([P, PAGES * DV // LIST_ROWS], U16, name="value_list")
-        steps = sb([P, P], F32, "steps")
-        distance = sb([P, P], F32, "distance")
-        kw_pool = sb([P, T], I32, "kw_pool")
+        one = at(16384 * 4 - 64, [P, 1216], F32, "one")
+        share = sb([P, 1], F32, "share")
+        kw_pool = at(16384 * 4 + 640 + 4096, [P, T], I32, "kw_pool")
         ks_pool = sb([P, T], U8, "ks_pool")
         kb_pool = at(0, [P, T], F32, "kb_pool")
-        vs_pool = at(16384, [P, T], F32, "vs_pool")
-        qw = sb([P, NQ], I32, "qw")
-        qs = sb([P, NQ], U8, "qs")
+        vs_pool = at(16384 * 3, [P, T], F32, "vs_pool")
+        qw = at(16384 * 4, [P, NQ], I32, "qw")
+        qs = at(16384 * 4 + 512, [P, NQ], U8, "qs")
         ident = sb([P, P], F32, "ident")
 
-        nc.gpsimd.memset(qs[:].bitcast(I32), 0)
-        nc.gpsimd.iota(steps[:], [[1, P]], base=0, channel_multiplier=-1, allow_small_or_imprecise_dtypes=True)
         nc.gpsimd.memset(ks_pool[:].bitcast(I32), 0)
-        nc.scalar.activation(distance[:], steps[:], ACT.Abs)
-        nc.scalar.activation(ident[:], distance[:], ACT.Relu, scale=-1.0, bias=1.0)
+        nc.gpsimd.memset(one[:, 0:1], 1.0)
+        nc.scalar.activation(share[:], one[:, 0:1], ACT.Identity, scale=1.0 / P)
         nc.vector.memset(kb_pool[0:BIAS_ROW, 0 : KB_SPLIT[0]], 0.0)
         nc.vector.memset(kb_pool[0:BIAS_ROW, KB_SPLIT[0] : KB_SPLIT[1]], 0.0)
         nc.gpsimd.memset(kb_pool[0:BIAS_ROW, KB_SPLIT[1] : T], 0.0)
+        nc.vector.memset(qs[:].bitcast(I32), 0)
         nc.vector.memset(vs_pool[0:BIAS_ROW, 0 : VS_SPLIT[0]], 0.0)
         nc.vector.memset(vs_pool[0:BIAS_ROW, VS_SPLIT[0] : VS_SPLIT[1]], 0.0)
         nc.gpsimd.memset(vs_pool[0:BIAS_ROW, VS_SPLIT[1] : T], 0.0)
@@ -78,32 +79,33 @@ def tile_attend_pkv8q_rel2_cap_kb_kernel(
         nc.sync.dma_start(key_list[:], offs)
         nc.sync.dma_start(kb_pool[BIAS_ROW:P, :], kb[0:1, :])
         nc.sync.dma_start(value_list[:], voffs)
+        for g in range(QUADRANTS):
+            nc.sync.dma_start(scale_rows(ks_pool, g), k_scales[0, 4 * g : 4 * g + 4, :].bitcast(I32))
+        key_words = k_words[0].rearrange("p t r -> p (t r)").bitcast(I32)
+        nc.sync.dma_start(kw_pool[:, 0:KW_FIRST], key_words[:, 0:KW_FIRST])
         nc.sync.dma_start(vs_pool[BIAS_ROW:P, :], vs[0:1, :])
+        nc.sync.dma_start(kw_pool[:, KW_FIRST:T], key_words[:, KW_FIRST:T])
         nc.sync.dma_start(qw[:], q_words[0, 0].rearrange("p q r -> p (q r)").bitcast(I32))
         for g in range(QUADRANTS):
-            if g == 2:
-                nc.sync.dma_start(kw_pool[:], k_words[0].rearrange("p t r -> p (t r)").bitcast(I32))
             nc.sync.dma_start(scale_rows(qs, g), q_scales[0, 0, 4 * g : 4 * g + 4, :].bitcast(I32))
-        for g in range(QUADRANTS):
-            nc.scalar.dma_start(scale_rows(ks_pool, g), k_scales[0, 4 * g : 4 * g + 4, :].bitcast(I32))
 
         def page_list(e):
             cols = PAGE // LIST_ROWS
             return key_list[:, e * cols : (e + 1) * cols]
 
-        def columns(name, pool, factor):
+        def columns(name, pool, factor, base):
             cols = []
             for e in range(PAGES):
                 row = sb([P, PAGE], F32, "%s_row%d" % (name, e))
                 nc.scalar.activation(row[:], pool[:].indirect(page_list(e)), ACT.Copy, scale=factor)
-                col = sb([P, PACK], F32, "%s_col%d" % (name, e))
+                col = at(base + 1024 * e, [P, PACK], F32, "%s_col%d" % (name, e))
                 nc.sync.dma_start(col[:], row[BIAS_ROW:P, :])
                 cols.append(col)
             return cols
 
-        kb_col = columns("kb", kb_pool, 1.0 / CAP)
+        kb_col = columns("kb", kb_pool, 1.0 / CAP, 45056 - 2048)
 
-        vw_pool = at(0, [P, POOL_PAGES * DV], I32, "vw_pool")
+        vw_pool = at(16384 * 4 + 640, [P, POOL_PAGES * DV], I32, "vw_pool")
         nc.sync.dma_start(
             vw_pool[:].rearrange("p (u e) -> p u e", u=POOL_PAGES),
             v_words.rearrange("u p e r -> p u (e r)").bitcast(I32),
@@ -115,7 +117,8 @@ def tile_attend_pkv8q_rel2_cap_kb_kernel(
                 scale_rows(vsc_pool, g).rearrange("p (u e) -> p u e", u=POOL_PAGES),
                 v_scales[:, 4 * g : 4 * g + 4, :].rearrange("u f e -> f u e").bitcast(I32),
             )
-        vs_col = columns("vs", vs_pool, CAP * CAP)
+        make_identity(nc, ident[:])
+        vs_col = columns("vs", vs_pool, CAP * CAP, 16384)
 
         ks_row = at(33792, [P, T], U8, "ks_row")[:, 0:N]
         nc.vector.tensor_copy(ks_row, ks_pool[:].indirect(key_list[:]))
@@ -124,7 +127,7 @@ def tile_attend_pkv8q_rel2_cap_kb_kernel(
 
         halves = [slice(h, h + HALF) for h in range(0, PACK, HALF)]
         capped = []
-        p_t = [sb([P, PACK, NQ], F32, "p%d" % e) for e in range(PAGES)]
+        p_t = [sb([P, PACK, NQ], F32, "p%d" % e) for e in range(PAGES - 1)]
 
         def square_on_scalar(e):
             pos = sb([P, PACK, NQ], F32, "pos0") if e == 0 else at(32768 + 4096, [P, PACK, NQ], F32, "pos1")
@@ -142,7 +145,7 @@ def tile_attend_pkv8q_rel2_cap_kb_kernel(
                     scores[t // HALF][:, t % HALF, :], lhsT=kw[:, t, :].bitcast(FP8X4), lhsT_scale=ks[:, t, e, :],
                     rhs=qw[:].bitcast(FP8X4), rhs_scale=qs[:], start=True, stop=True,
                 )
-            capped.append(at(16384 + 2048 * e, [P, PACK, NQ], F32, "capped%d" % e))
+            capped.append(at(16384 * 3 + 2048 * e, [P, PACK, NQ], F32, "capped%d" % e))
             for t in range(PACK):
                 nc.scalar.activation(
                     capped[e][:, t, :], scores[t // HALF][:, t % HALF, :], ACT.Tanh,
@@ -169,6 +172,7 @@ def tile_attend_pkv8q_rel2_cap_kb_kernel(
             )
 
         weights(0)
+        p_t.append(at(4096, [P, PACK, NQ], F32, "p2"))
         nc.vector.scalar_tensor_tensor(p_t[2][:], capped[2][:], 0.0, capped[2][:], ALU.max, ALU.mult)
         weights(2)
         weights(1)
@@ -183,11 +187,9 @@ def tile_attend_pkv8q_rel2_cap_kb_kernel(
                 )
         parts = sb([P, P], F32, "parts")
         denom = sb([P, 1], F32, "denom")
-        nc.scalar.activation(parts[:], total[:], ACT.Copy, scale=CAP * CAP, bias=1.0 / P, accum_out=denom[:])
-        inv = sb([P, 1], F32, "inv")
-        nc.vector.reciprocal(inv[:], denom[:])
+        nc.scalar.activation(parts[:], total[:], ACT.Identity, scale=CAP * CAP, bias=share[:], accum_out=denom[:])
         for e in order:
-            w_codes = sb([P, NQ], U32, "w_codes%d" % e)
+            w_codes = at({0: 45056, 2: 32768 + 4096, 1: 49152}[e], [P, NQ], U32, "w_codes%d" % e)
             w_scales = sb([P, NQ], U8, "w_scales%d" % e)
             nc.vector.quantize_mx(w_codes[:].bitcast(FP8X4), w_scales[:], w[e][:])
             cols = slice(e * DV, (e + 1) * DV)
@@ -197,6 +199,8 @@ def tile_attend_pkv8q_rel2_cap_kb_kernel(
                 start=(e == order[0]), stop=(e == order[-1]),
             )
 
+        inv = sb([P, 1], F32, "inv", "p1")
+        nc.vector.reciprocal(inv[:], denom[:])
         y = sb([P, DV], F32, "y")
         nc.scalar.activation(y[:], acc[:], ACT.Copy, scale=inv[:])
         nc.sync.dma_start(out[0], y[:])

@@ -16,7 +16,6 @@ BIAS_ROW = P - 1
 HALF = 2
 PAIR = 2
 
-KW_FIRST = 1024
 KB_SPLIT = (1161, 2320)
 VS_SPLIT = (545, 1088)
 
@@ -55,7 +54,7 @@ def tile_attend_pkv8q_rel2_cap_kb_kernel(
 
         key_list = lists.tile([P, N // LIST_ROWS], U16, name="key_list")
         value_list = lists.tile([P, PAGES * DV // LIST_ROWS], U16, name="value_list")
-        one = at(16384 * 4 - 64, [P, 1216], F32, "one")
+        one = at(16384 * 4, [P, 1200], F32, "one")
         share = sb([P, 1], F32, "share")
         kw_pool = at(16384 * 4 + 640 + 4096, [P, T], I32, "kw_pool")
         ks_pool = sb([P, T], U8, "ks_pool")
@@ -78,13 +77,11 @@ def tile_attend_pkv8q_rel2_cap_kb_kernel(
 
         nc.sync.dma_start(key_list[:], offs)
         nc.sync.dma_start(kb_pool[BIAS_ROW:P, :], kb[0:1, :])
+        nc.sync.dma_start(vs_pool[BIAS_ROW:P, :], vs[0:1, :])
         nc.sync.dma_start(value_list[:], voffs)
         for g in range(QUADRANTS):
             nc.sync.dma_start(scale_rows(ks_pool, g), k_scales[0, 4 * g : 4 * g + 4, :].bitcast(I32))
-        key_words = k_words[0].rearrange("p t r -> p (t r)").bitcast(I32)
-        nc.sync.dma_start(kw_pool[:, 0:KW_FIRST], key_words[:, 0:KW_FIRST])
-        nc.sync.dma_start(vs_pool[BIAS_ROW:P, :], vs[0:1, :])
-        nc.sync.dma_start(kw_pool[:, KW_FIRST:T], key_words[:, KW_FIRST:T])
+        nc.sync.dma_start(kw_pool[:], k_words[0].rearrange("p t r -> p (t r)").bitcast(I32))
         nc.sync.dma_start(qw[:], q_words[0, 0].rearrange("p q r -> p (q r)").bitcast(I32))
         for g in range(QUADRANTS):
             nc.sync.dma_start(scale_rows(qs, g), q_scales[0, 0, 4 * g : 4 * g + 4, :].bitcast(I32))
@@ -120,10 +117,16 @@ def tile_attend_pkv8q_rel2_cap_kb_kernel(
         make_identity(nc, ident[:])
         vs_col = columns("vs", vs_pool, CAP * CAP, 16384)
 
-        ks_row = at(33792, [P, T], U8, "ks_row")[:, 0:N]
-        nc.vector.tensor_copy(ks_row, ks_pool[:].indirect(key_list[:]))
-        ks = sb([P, PACK, PAGES, P], U8, "ks")
-        nc.vector.tensor_copy(ks[:], ks_row.rearrange("p (e s t) -> p t e s", e=PAGES, t=PACK))
+        cols = PAGE // LIST_ROWS
+        groups = ((0, 2), (2, 1))
+        rows = [at(33792, [P, T], U8, "ks_row0")[:, 0 : 2 * PAGE], sb([P, PAGE], U8, "ks_row1")[:]]
+        for (first, count), row in zip(groups, rows):
+            nc.vector.tensor_copy(row, ks_pool[:].indirect(key_list[:, first * cols : (first + count) * cols]))
+        ks = []
+        for (first, count), row in zip(groups, rows):
+            dealt = sb([P, PACK, count, P], U8, "ks%d" % first)
+            nc.vector.tensor_copy(dealt[:], row.rearrange("p (e s t) -> p t e s", e=count, t=PACK))
+            ks.extend(dealt[:, :, e, :] for e in range(count))
 
         halves = [slice(h, h + HALF) for h in range(0, PACK, HALF)]
         capped = []
@@ -142,7 +145,7 @@ def tile_attend_pkv8q_rel2_cap_kb_kernel(
             scores = [psum.tile([P, HALF, NQ], F32, name="scores%d_%d" % (e, h)) for h in range(PACK // HALF)]
             for t in range(PACK):
                 nc.tensor.matmul_mx(
-                    scores[t // HALF][:, t % HALF, :], lhsT=kw[:, t, :].bitcast(FP8X4), lhsT_scale=ks[:, t, e, :],
+                    scores[t // HALF][:, t % HALF, :], lhsT=kw[:, t, :].bitcast(FP8X4), lhsT_scale=ks[e][:, t, :],
                     rhs=qw[:].bitcast(FP8X4), rhs_scale=qs[:], start=True, stop=True,
                 )
             capped.append(at(16384 * 3 + 2048 * e, [P, PACK, NQ], F32, "capped%d" % e))

@@ -16,8 +16,9 @@ BIAS_ROW = P - 1
 HALF = 2
 PAIR = 2
 
-KB_SPLIT = (1161, 2320)
-VS_SPLIT = (545, 1088)
+KW_FIRST = 1024
+KS_SPLIT = 400
+VS_SPLIT = 1800
 
 FLOPS = 2 * NQ * N * D + 2 * NQ * N * DV
 BYTES = (T * D + T * DV + NQ * D) * 33 // 32 + 2 * 4 * T + 2 * P * (N + PAGES * DV) // LIST_ROWS + 4 * NQ * DV
@@ -54,7 +55,7 @@ def tile_attend_pkv8q_rel2_cap_kb_kernel(
 
         key_list = lists.tile([P, N // LIST_ROWS], U16, name="key_list")
         value_list = lists.tile([P, PAGES * DV // LIST_ROWS], U16, name="value_list")
-        one = at(16384 * 4, [P, 1200], F32, "one")
+        one = at(16384 * 4 - 64, [P, 1216], F32, "one")
         share = sb([P, 1], F32, "share")
         kw_pool = at(16384 * 4 + 640 + 4096, [P, T], I32, "kw_pool")
         ks_pool = sb([P, T], U8, "ks_pool")
@@ -62,26 +63,25 @@ def tile_attend_pkv8q_rel2_cap_kb_kernel(
         vs_pool = at(16384 * 3, [P, T], F32, "vs_pool")
         qw = at(16384 * 4, [P, NQ], I32, "qw")
         qs = at(16384 * 4 + 512, [P, NQ], U8, "qs")
-        ident = sb([P, P], F32, "ident")
 
-        nc.gpsimd.memset(ks_pool[:].bitcast(I32), 0)
-        nc.gpsimd.memset(one[:, 0:1], 1.0)
+        nc.gpsimd.memset(ks_pool[:].bitcast(I32)[:, 0:KS_SPLIT], 0)
+        nc.vector.memset(ks_pool[:].bitcast(I32)[:, KS_SPLIT : T // 4], 0)
+        nc.vector.memset(one[:, 0:1], 1.0)
         nc.scalar.activation(share[:], one[:, 0:1], ACT.Identity, scale=1.0 / P)
-        nc.vector.memset(kb_pool[0:BIAS_ROW, 0 : KB_SPLIT[0]], 0.0)
-        nc.vector.memset(kb_pool[0:BIAS_ROW, KB_SPLIT[0] : KB_SPLIT[1]], 0.0)
-        nc.gpsimd.memset(kb_pool[0:BIAS_ROW, KB_SPLIT[1] : T], 0.0)
-        nc.vector.memset(qs[:].bitcast(I32), 0)
-        nc.vector.memset(vs_pool[0:BIAS_ROW, 0 : VS_SPLIT[0]], 0.0)
-        nc.vector.memset(vs_pool[0:BIAS_ROW, VS_SPLIT[0] : VS_SPLIT[1]], 0.0)
-        nc.gpsimd.memset(vs_pool[0:BIAS_ROW, VS_SPLIT[1] : T], 0.0)
+        nc.vector.memset(kb_pool[0:BIAS_ROW, :], 0.0)
+        nc.gpsimd.memset(qs[:].bitcast(I32), 0)
+        nc.vector.memset(vs_pool[0:BIAS_ROW, 0:VS_SPLIT], 0.0)
+        nc.gpsimd.memset(vs_pool[0:BIAS_ROW, VS_SPLIT:T], 0.0)
 
         nc.sync.dma_start(key_list[:], offs)
         nc.sync.dma_start(kb_pool[BIAS_ROW:P, :], kb[0:1, :])
-        nc.sync.dma_start(vs_pool[BIAS_ROW:P, :], vs[0:1, :])
         nc.sync.dma_start(value_list[:], voffs)
         for g in range(QUADRANTS):
             nc.sync.dma_start(scale_rows(ks_pool, g), k_scales[0, 4 * g : 4 * g + 4, :].bitcast(I32))
-        nc.sync.dma_start(kw_pool[:], k_words[0].rearrange("p t r -> p (t r)").bitcast(I32))
+        key_words = k_words[0].rearrange("p t r -> p (t r)").bitcast(I32)
+        nc.sync.dma_start(kw_pool[:, 0:KW_FIRST], key_words[:, 0:KW_FIRST])
+        nc.sync.dma_start(vs_pool[BIAS_ROW:P, :], vs[0:1, :])
+        nc.sync.dma_start(kw_pool[:, KW_FIRST:T], key_words[:, KW_FIRST:T])
         nc.sync.dma_start(qw[:], q_words[0, 0].rearrange("p q r -> p (q r)").bitcast(I32))
         for g in range(QUADRANTS):
             nc.sync.dma_start(scale_rows(qs, g), q_scales[0, 0, 4 * g : 4 * g + 4, :].bitcast(I32))
@@ -114,6 +114,7 @@ def tile_attend_pkv8q_rel2_cap_kb_kernel(
                 scale_rows(vsc_pool, g).rearrange("p (u e) -> p u e", u=POOL_PAGES),
                 v_scales[:, 4 * g : 4 * g + 4, :].rearrange("u f e -> f u e").bitcast(I32),
             )
+        ident = at(8192, [P, P], F32, "ident")
         make_identity(nc, ident[:])
         vs_col = columns("vs", vs_pool, CAP * CAP, 16384)
 

@@ -16,8 +16,8 @@ BIAS_ROW = P - 1
 HALF = 2
 PAIR = 2
 
-KW_FIRST = 1024
-KS_SPLIT = 400
+KW_FIRST = 1280
+KS_SPLIT = 304
 VS_SPLIT = 1800
 
 FLOPS = 2 * NQ * N * D + 2 * NQ * N * DV
@@ -57,7 +57,7 @@ def tile_attend_pkv8q_rel2_cap_kb_kernel(
         value_list = lists.tile([P, PAGES * DV // LIST_ROWS], U16, name="value_list")
         one = at(16384 * 4 - 64, [P, 1216], F32, "one")
         share = sb([P, 1], F32, "share")
-        kw_pool = at(16384 * 4 + 640 + 4096, [P, T], I32, "kw_pool")
+        kw_pool = at(16384 * 5, [P, T], I32, "kw_pool")
         ks_pool = sb([P, T], U8, "ks_pool")
         kb_pool = at(0, [P, T], F32, "kb_pool")
         vs_pool = at(16384 * 3, [P, T], F32, "vs_pool")
@@ -76,10 +76,10 @@ def tile_attend_pkv8q_rel2_cap_kb_kernel(
         nc.sync.dma_start(key_list[:], offs)
         nc.sync.dma_start(kb_pool[BIAS_ROW:P, :], kb[0:1, :])
         nc.sync.dma_start(value_list[:], voffs)
-        for g in range(QUADRANTS):
-            nc.sync.dma_start(scale_rows(ks_pool, g), k_scales[0, 4 * g : 4 * g + 4, :].bitcast(I32))
         key_words = k_words[0].rearrange("p t r -> p (t r)").bitcast(I32)
         nc.sync.dma_start(kw_pool[:, 0:KW_FIRST], key_words[:, 0:KW_FIRST])
+        for g in range(QUADRANTS):
+            nc.sync.dma_start(scale_rows(ks_pool, g), k_scales[0, 4 * g : 4 * g + 4, :].bitcast(I32))
         nc.sync.dma_start(vs_pool[BIAS_ROW:P, :], vs[0:1, :])
         nc.sync.dma_start(kw_pool[:, KW_FIRST:T], key_words[:, KW_FIRST:T])
         nc.sync.dma_start(qw[:], q_words[0, 0].rearrange("p q r -> p (q r)").bitcast(I32))

@@ -50,8 +50,8 @@ def tile_attend_pkv8q_rel2_cap_kb_kernel(
         def at(offset, shape, dtype, name):
             return placed.tile(shape, dtype, name=name, align_bytes=64, offset=offset)
 
-        def scale_rows(plane, g):
-            return plane[32 * g : 32 * g + 4, :].bitcast(I32)
+        def scale_rows(plane, r):
+            return plane[r:P:32, :].bitcast(I32)
 
         key_list = lists.tile([P, N // LIST_ROWS], U16, name="key_list")
         value_list = lists.tile([P, PAGES * DV // LIST_ROWS], U16, name="value_list")
@@ -79,12 +79,12 @@ def tile_attend_pkv8q_rel2_cap_kb_kernel(
         key_words = k_words[0].rearrange("p t r -> p (t r)").bitcast(I32)
         nc.sync.dma_start(kw_pool[:, 0:KW_FIRST], key_words[:, 0:KW_FIRST])
         for g in range(QUADRANTS):
-            nc.sync.dma_start(scale_rows(ks_pool, g), k_scales[0, 4 * g : 4 * g + 4, :].bitcast(I32))
+            nc.sync.dma_start(scale_rows(ks_pool, g), k_scales[0].rearrange("(a r) t -> r a t", r=4)[g].bitcast(I32))
         nc.sync.dma_start(vs_pool[BIAS_ROW:P, :], vs[0:1, :])
         nc.sync.dma_start(kw_pool[:, KW_FIRST:T], key_words[:, KW_FIRST:T])
         nc.sync.dma_start(qw[:], q_words[0, 0].rearrange("p q r -> p (q r)").bitcast(I32))
         for g in range(QUADRANTS):
-            nc.sync.dma_start(scale_rows(qs, g), q_scales[0, 0, 4 * g : 4 * g + 4, :].bitcast(I32))
+            nc.sync.dma_start(scale_rows(qs, g), q_scales[0, 0].rearrange("(a r) q -> r a q", r=4)[g].bitcast(I32))
 
         def page_list(e):
             cols = PAGE // LIST_ROWS
@@ -112,7 +112,7 @@ def tile_attend_pkv8q_rel2_cap_kb_kernel(
         for g in range(QUADRANTS):
             nc.sync.dma_start(
                 scale_rows(vsc_pool, g).rearrange("p (u e) -> p u e", u=POOL_PAGES),
-                v_scales[:, 4 * g : 4 * g + 4, :].rearrange("u f e -> f u e").bitcast(I32),
+                v_scales.rearrange("u (a r) e -> r a u e", r=4)[g].bitcast(I32),
             )
         ident = at(8192, [P, P], F32, "ident")
         make_identity(nc, ident[:])

@@ -16,9 +16,11 @@ BIAS_ROW = P - 1
 HALF = 2
 PAIR = 2
 
-KW_FIRST = 1280
-KS_SPLIT = 304
-VS_SPLIT = 1800
+
+KS_SPLIT = 600
+KB_SPLIT = 2400
+VS_SPLIT = 1504
+KW_CUTS = (0, 832, 2688, T)
 
 FLOPS = 2 * NQ * N * D + 2 * NQ * N * DV
 BYTES = (T * D + T * DV + NQ * D) * 33 // 32 + 2 * 4 * T + 2 * P * (N + PAGES * DV) // LIST_ROWS + 4 * NQ * DV
@@ -53,38 +55,52 @@ def tile_attend_pkv8q_rel2_cap_kb_kernel(
         def scale_rows(plane, r):
             return plane[r:P:32, :].bitcast(I32)
 
+        KB_AT, COLS_AT, KEYS_AT, VS_AT, Q_AT, KW_AT = 0, 16384, 32768, 49152, 65536, 81920
+
         key_list = lists.tile([P, N // LIST_ROWS], U16, name="key_list")
         value_list = lists.tile([P, PAGES * DV // LIST_ROWS], U16, name="value_list")
-        one = at(16384 * 4 - 64, [P, 1216], F32, "one")
+        one = sb([P, 1], F32, "one")
         share = sb([P, 1], F32, "share")
-        kw_pool = at(16384 * 5, [P, T], I32, "kw_pool")
+        kw_pool = at(KW_AT, [P, T], I32, "kw_pool")
         ks_pool = sb([P, T], U8, "ks_pool")
-        kb_pool = at(0, [P, T], F32, "kb_pool")
-        vs_pool = at(16384 * 3, [P, T], F32, "vs_pool")
-        qw = at(16384 * 4, [P, NQ], I32, "qw")
-        qs = at(16384 * 4 + 512, [P, NQ], U8, "qs")
+        kb_pool = at(KB_AT, [P, T], F32, "kb_pool")
+        vs_pool = at(VS_AT, [P, T], F32, "vs_pool")
+        qw = at(Q_AT, [P, NQ], I32, "qw")
+        qs = at(Q_AT + 512, [P, NQ], U8, "qs")
+
+        def zero_on_vector(pool, first, last):
+            middle = first + (last - first) // 4 * 2 + 1
+            nc.vector.memset(pool[:, first:middle], 0)
+            nc.vector.memset(pool[:, middle:last], 0)
 
         nc.gpsimd.memset(ks_pool[:].bitcast(I32)[:, 0:KS_SPLIT], 0)
-        nc.vector.memset(ks_pool[:].bitcast(I32)[:, KS_SPLIT : T // 4], 0)
-        nc.vector.memset(one[:, 0:1], 1.0)
-        nc.scalar.activation(share[:], one[:, 0:1], ACT.Identity, scale=1.0 / P)
-        nc.vector.memset(kb_pool[0:BIAS_ROW, :], 0.0)
+        zero_on_vector(ks_pool[:].bitcast(I32), KS_SPLIT, T // 4)
+        nc.vector.memset(one[:], 1.0)
+        nc.scalar.activation(share[:], one[:], ACT.Identity, scale=1.0 / P)
         nc.gpsimd.memset(qs[:].bitcast(I32), 0)
-        nc.vector.memset(vs_pool[0:BIAS_ROW, 0:VS_SPLIT], 0.0)
+        zero_on_vector(kb_pool[0:BIAS_ROW, :], 0, KB_SPLIT)
+        nc.gpsimd.memset(kb_pool[0:BIAS_ROW, KB_SPLIT:T], 0.0)
+        zero_on_vector(vs_pool[0:BIAS_ROW, :], 0, VS_SPLIT)
         nc.gpsimd.memset(vs_pool[0:BIAS_ROW, VS_SPLIT:T], 0.0)
+
+        key_words = k_words[0].rearrange("p t r -> p (t r)").bitcast(I32)
+
+        def load_keys(i):
+            part = slice(KW_CUTS[i], KW_CUTS[i + 1])
+            nc.sync.dma_start(kw_pool[:, part], key_words[:, part])
 
         nc.sync.dma_start(key_list[:], offs)
         nc.sync.dma_start(kb_pool[BIAS_ROW:P, :], kb[0:1, :])
         nc.sync.dma_start(value_list[:], voffs)
-        key_words = k_words[0].rearrange("p t r -> p (t r)").bitcast(I32)
-        nc.sync.dma_start(kw_pool[:, 0:KW_FIRST], key_words[:, 0:KW_FIRST])
+        load_keys(0)
         for g in range(QUADRANTS):
             nc.sync.dma_start(scale_rows(ks_pool, g), k_scales[0].rearrange("(a r) t -> r a t", r=4)[g].bitcast(I32))
         nc.sync.dma_start(vs_pool[BIAS_ROW:P, :], vs[0:1, :])
-        nc.sync.dma_start(kw_pool[:, KW_FIRST:T], key_words[:, KW_FIRST:T])
+        load_keys(1)
         nc.sync.dma_start(qw[:], q_words[0, 0].rearrange("p q r -> p (q r)").bitcast(I32))
         for g in range(QUADRANTS):
             nc.sync.dma_start(scale_rows(qs, g), q_scales[0, 0].rearrange("(a r) q -> r a q", r=4)[g].bitcast(I32))
+        load_keys(2)
 
         def page_list(e):
             cols = PAGE // LIST_ROWS
@@ -102,25 +118,23 @@ def tile_attend_pkv8q_rel2_cap_kb_kernel(
 
         kb_col = columns("kb", kb_pool, 1.0 / CAP, 45056 - 2048)
 
-        vw_pool = at(16384 * 4 + 640, [P, POOL_PAGES * DV], I32, "vw_pool")
+        vw_pool = at(KB_AT + 8192, [P, POOL_PAGES * DV], I32, "vw_pool")
         nc.sync.dma_start(
             vw_pool[:].rearrange("p (u e) -> p u e", u=POOL_PAGES),
             v_words.rearrange("u p e r -> p u (e r)").bitcast(I32),
         )
-        vsc_pool = at(4096, [P, POOL_PAGES * DV], U8, "vsc_pool")
+        vsc_pool = at(KB_AT + 4096, [P, POOL_PAGES * DV], U8, "vsc_pool")
         nc.gpsimd.memset(vsc_pool[:].bitcast(I32), 0)
         for g in range(QUADRANTS):
             nc.sync.dma_start(
                 scale_rows(vsc_pool, g).rearrange("p (u e) -> p u e", u=POOL_PAGES),
                 v_scales.rearrange("u (a r) e -> r a u e", r=4)[g].bitcast(I32),
             )
-        ident = at(8192, [P, P], F32, "ident")
-        make_identity(nc, ident[:])
-        vs_col = columns("vs", vs_pool, CAP * CAP, 16384)
+        vs_col = columns("vs", vs_pool, CAP * CAP, COLS_AT)
 
         cols = PAGE // LIST_ROWS
         groups = ((0, 2), (2, 1))
-        rows = [at(33792, [P, T], U8, "ks_row0")[:, 0 : 2 * PAGE], sb([P, PAGE], U8, "ks_row1")[:]]
+        rows = [at(KEYS_AT + 1024, [P, 6144], U8, "ks_row0")[:, 0 : 2 * PAGE], sb([P, PAGE], U8, "ks_row1")[:]]
         for (first, count), row in zip(groups, rows):
             nc.vector.tensor_copy(row, ks_pool[:].indirect(key_list[:, first * cols : (first + count) * cols]))
         ks = []
@@ -128,20 +142,21 @@ def tile_attend_pkv8q_rel2_cap_kb_kernel(
             dealt = sb([P, PACK, count, P], U8, "ks%d" % first)
             nc.vector.tensor_copy(dealt[:], row.rearrange("p (e s t) -> p t e s", e=count, t=PACK))
             ks.extend(dealt[:, :, e, :] for e in range(count))
+        ident = at(KEYS_AT + 6144, [P, P], F32, "ident")
+        make_identity(nc, ident[:])
 
         halves = [slice(h, h + HALF) for h in range(0, PACK, HALF)]
         capped = []
         p_t = [sb([P, PACK, NQ], F32, "p%d" % e) for e in range(PAGES - 1)]
 
-        def square_on_scalar(e):
-            pos = sb([P, PACK, NQ], F32, "pos0") if e == 0 else at(32768 + 4096, [P, PACK, NQ], F32, "pos1")
+        def square_on_scalar(e, pos):
             for h in halves:
                 nc.scalar.activation(pos[:, h, :], capped[e][:, h, :], ACT.Relu)
             for h in halves:
                 nc.scalar.activation(p_t[e][:, h, :], pos[:, h, :], ACT.Square)
 
         for e in range(PAGES):
-            kw = at(32768 + 2048 * e, [P, PACK, P], U32, "kw%d" % e)
+            kw = at(KEYS_AT + 2048 * e, [P, PACK, P], U32, "kw%d" % e)
             nc.vector.tensor_copy(kw[:].rearrange("p t s -> p s t"), kw_pool[:].bitcast(U32).indirect(page_list(e)))
             scores = [psum.tile([P, HALF, NQ], F32, name="scores%d_%d" % (e, h)) for h in range(PACK // HALF)]
             for t in range(PACK):
@@ -149,22 +164,21 @@ def tile_attend_pkv8q_rel2_cap_kb_kernel(
                     scores[t // HALF][:, t % HALF, :], lhsT=kw[:, t, :].bitcast(FP8X4), lhsT_scale=ks[e][:, t, :],
                     rhs=qw[:].bitcast(FP8X4), rhs_scale=qs[:], start=True, stop=True,
                 )
-            capped.append(at(16384 * 3 + 2048 * e, [P, PACK, NQ], F32, "capped%d" % e))
+            capped.append(at(VS_AT + 2048 * e, [P, PACK, NQ], F32, "capped%d" % e))
             for t in range(PACK):
                 nc.scalar.activation(
                     capped[e][:, t, :], scores[t // HALF][:, t % HALF, :], ACT.Tanh,
                     scale=1.0 / CAP, bias=kb_col[e][:, t : t + 1],
                 )
             if e == 0:
-                square_on_scalar(0)
-        square_on_scalar(1)
+                square_on_scalar(0, sb([P, PACK, NQ], F32, "pos0"))
+        square_on_scalar(1, at(KEYS_AT + 4096, [P, PACK, NQ], F32, "pos1"))
 
-        vw = at(32768, [P, PAGES * DV], U32, "vw")
+        vw = at(KEYS_AT, [P, PAGES * DV], U32, "vw")
         nc.vector.tensor_copy(vw[:], vw_pool[:].bitcast(U32).indirect(value_list[:]))
-        vsc = at(32768 + 1536, [P, PAGES * DV], U8, "vsc")
+        vsc = at(KEYS_AT + 1536, [P, PAGES * DV], U8, "vsc")
         nc.vector.tensor_copy(vsc[:], vsc_pool[:].indirect(value_list[:]))
 
-        order = (0, 2, 1)
         w = [sb([P, NQ * PACK], BF16, "w%d" % e) for e in range(PAGES)]
 
         def weights(e):
@@ -176,11 +190,12 @@ def tile_attend_pkv8q_rel2_cap_kb_kernel(
             )
 
         weights(0)
-        p_t.append(at(4096, [P, PACK, NQ], F32, "p2"))
+        p_t.append(at(KB_AT + 4096, [P, PACK, NQ], F32, "p2"))
         nc.vector.scalar_tensor_tensor(p_t[2][:], capped[2][:], 0.0, capped[2][:], ALU.max, ALU.mult)
         weights(2)
         weights(1)
 
+        order = (0, 2, 1)
         total = psum.tile([P, P], F32, name="total")
         acc = psum.tile([P, DV], F32, name="acc")
         for e in order:

@@ -17,9 +17,7 @@ HALF = 2
 PAIR = 2
 
 
-KS_SPLIT = 600
-KB_SPLIT = 2400
-VS_SPLIT = 1504
+KS_SPLIT = 304
 KW_CUTS = (0, 832, 2688, T)
 
 FLOPS = 2 * NQ * N * D + 2 * NQ * N * DV
@@ -68,20 +66,13 @@ def tile_attend_pkv8q_rel2_cap_kb_kernel(
         qw = at(Q_AT, [P, NQ], I32, "qw")
         qs = at(Q_AT + 512, [P, NQ], U8, "qs")
 
-        def zero_on_vector(pool, first, last):
-            middle = first + (last - first) // 4 * 2 + 1
-            nc.vector.memset(pool[:, first:middle], 0)
-            nc.vector.memset(pool[:, middle:last], 0)
-
         nc.gpsimd.memset(ks_pool[:].bitcast(I32)[:, 0:KS_SPLIT], 0)
-        zero_on_vector(ks_pool[:].bitcast(I32), KS_SPLIT, T // 4)
+        nc.gpsimd.memset(qs[:].bitcast(I32), 0)
+        nc.vector.memset(ks_pool[:].bitcast(I32)[:, KS_SPLIT : T // 4], 0)
         nc.vector.memset(one[:], 1.0)
         nc.scalar.activation(share[:], one[:], ACT.Identity, scale=1.0 / P)
-        nc.gpsimd.memset(qs[:].bitcast(I32), 0)
-        zero_on_vector(kb_pool[0:BIAS_ROW, :], 0, KB_SPLIT)
-        nc.gpsimd.memset(kb_pool[0:BIAS_ROW, KB_SPLIT:T], 0.0)
-        zero_on_vector(vs_pool[0:BIAS_ROW, :], 0, VS_SPLIT)
-        nc.gpsimd.memset(vs_pool[0:BIAS_ROW, VS_SPLIT:T], 0.0)
+        nc.vector.memset(kb_pool[0:BIAS_ROW, :], 0.0)
+        nc.vector.memset(vs_pool[0:BIAS_ROW, :], 0.0)
 
         key_words = k_words[0].rearrange("p t r -> p (t r)").bitcast(I32)
 
@@ -132,16 +123,20 @@ def tile_attend_pkv8q_rel2_cap_kb_kernel(
             )
         vs_col = columns("vs", vs_pool, CAP * CAP, COLS_AT)
 
-        cols = PAGE // LIST_ROWS
-        groups = ((0, 2), (2, 1))
-        rows = [at(KEYS_AT + 1024, [P, 6144], U8, "ks_row0")[:, 0 : 2 * PAGE], sb([P, PAGE], U8, "ks_row1")[:]]
-        for (first, count), row in zip(groups, rows):
-            nc.vector.tensor_copy(row, ks_pool[:].indirect(key_list[:, first * cols : (first + count) * cols]))
-        ks = []
-        for (first, count), row in zip(groups, rows):
-            dealt = sb([P, PACK, count, P], U8, "ks%d" % first)
-            nc.vector.tensor_copy(dealt[:], row.rearrange("p (e s t) -> p t e s", e=count, t=PACK))
-            ks.extend(dealt[:, :, e, :] for e in range(count))
+        def gather_scales(e, row):
+            nc.vector.tensor_copy(row, ks_pool[:].indirect(page_list(e)))
+            return row
+
+        def deal_scales(e, row):
+            dealt = sb([P, PACK, P], U8, "ks%d" % e)
+            nc.vector.tensor_copy(dealt[:], row.rearrange("p (s t) -> p t s", t=PACK))
+            return dealt
+
+        rows = [
+            gather_scales(0, sb([P, PAGE], U8, "ks_row0")[:]),
+            gather_scales(1, at(KEYS_AT, [P, 8192], U8, "ks_row1")[:, 0:PAGE]),
+        ]
+        ks = [deal_scales(e, row) for e, row in enumerate(rows)]
         ident = at(KEYS_AT + 6144, [P, P], F32, "ident")
         make_identity(nc, ident[:])
 
@@ -156,8 +151,12 @@ def tile_attend_pkv8q_rel2_cap_kb_kernel(
                 nc.scalar.activation(p_t[e][:, h, :], pos[:, h, :], ACT.Square)
 
         for e in range(PAGES):
-            kw = at(KEYS_AT + 2048 * e, [P, PACK, P], U32, "kw%d" % e)
+            if e == PAGES - 1:
+                row = gather_scales(e, at(KEYS_AT, [P, PAGE], U8, "ks_row2")[:])
+            kw = at(KEYS_AT + (0, 4096, 512)[e], [P, PACK, P], U32, "kw%d" % e)
             nc.vector.tensor_copy(kw[:].rearrange("p t s -> p s t"), kw_pool[:].bitcast(U32).indirect(page_list(e)))
+            if e == PAGES - 1:
+                ks.append(deal_scales(e, row))
             scores = [psum.tile([P, HALF, NQ], F32, name="scores%d_%d" % (e, h)) for h in range(PACK // HALF)]
             for t in range(PACK):
                 nc.tensor.matmul_mx(
@@ -172,11 +171,11 @@ def tile_attend_pkv8q_rel2_cap_kb_kernel(
                 )
             if e == 0:
                 square_on_scalar(0, sb([P, PACK, NQ], F32, "pos0"))
-        square_on_scalar(1, at(KEYS_AT + 4096, [P, PACK, NQ], F32, "pos1"))
+        square_on_scalar(1, at(KEYS_AT + 512, [P, PACK, NQ], F32, "pos1"))
 
-        vw = at(KEYS_AT, [P, PAGES * DV], U32, "vw")
+        vw = at(KEYS_AT + 4096, [P, PAGES * DV], U32, "vw")
         nc.vector.tensor_copy(vw[:], vw_pool[:].bitcast(U32).indirect(value_list[:]))
-        vsc = at(KEYS_AT + 1536, [P, PAGES * DV], U8, "vsc")
+        vsc = at(KEYS_AT + 4096 + 1536, [P, PAGES * DV], U8, "vsc")
         nc.vector.tensor_copy(vsc[:], vsc_pool[:].indirect(value_list[:]))
 
         w = [sb([P, NQ * PACK], BF16, "w%d" % e) for e in range(PAGES)]
@@ -196,7 +195,7 @@ def tile_attend_pkv8q_rel2_cap_kb_kernel(
         weights(1)
 
         order = (0, 2, 1)
-        total = psum.tile([P, P], F32, name="total")
+        total = psum.tile([P, P], F32, name="total", tag="scores1_1")
         acc = psum.tile([P, DV], F32, name="acc")
         for e in order:
             for t in range(PACK):
@@ -208,7 +207,7 @@ def tile_attend_pkv8q_rel2_cap_kb_kernel(
         denom = sb([P, 1], F32, "denom")
         nc.scalar.activation(parts[:], total[:], ACT.Identity, scale=CAP * CAP, bias=share[:], accum_out=denom[:])
         for e in order:
-            w_codes = at({0: 45056, 2: 32768 + 4096, 1: 49152}[e], [P, NQ], U32, "w_codes%d" % e)
+            w_codes = at({0: 45056, 2: KEYS_AT + 512, 1: 49152}[e], [P, NQ], U32, "w_codes%d" % e)
             w_scales = sb([P, NQ], U8, "w_scales%d" % e)
             nc.vector.quantize_mx(w_codes[:].bitcast(FP8X4), w_scales[:], w[e][:])
             cols = slice(e * DV, (e + 1) * DV)

@@ -18,6 +18,7 @@ PAIR = 2
 
 
 KS_SPLIT = 304
+VS_SPLIT = 3000
 KW_CUTS = (0, 832, 2688, T)
 
 FLOPS = 2 * NQ * N * D + 2 * NQ * N * DV
@@ -53,26 +54,27 @@ def tile_attend_pkv8q_rel2_cap_kb_kernel(
         def scale_rows(plane, r):
             return plane[r:P:32, :].bitcast(I32)
 
-        KB_AT, COLS_AT, KEYS_AT, VS_AT, Q_AT, KW_AT = 0, 16384, 32768, 49152, 65536, 81920
+        KB_AT, COLS_AT, POS_AT, KEYS_AT, VS_AT, Q_AT, KW_AT = 0, 16384, 20480, 32768, 49152, 65536, 81920
 
         key_list = lists.tile([P, N // LIST_ROWS], U16, name="key_list")
         value_list = lists.tile([P, PAGES * DV // LIST_ROWS], U16, name="value_list")
-        one = sb([P, 1], F32, "one")
+        one = at(Q_AT - 64, [P, 32], F32, "one")
         share = sb([P, 1], F32, "share")
         kw_pool = at(KW_AT, [P, T], I32, "kw_pool")
         ks_pool = sb([P, T], U8, "ks_pool")
         kb_pool = at(KB_AT, [P, T], F32, "kb_pool")
         vs_pool = at(VS_AT, [P, T], F32, "vs_pool")
-        qw = at(Q_AT, [P, NQ], I32, "qw")
-        qs = at(Q_AT + 512, [P, NQ], U8, "qs")
+        qw = sb([P, NQ], I32, "qw")
+        qs = at(Q_AT, [P, NQ], U8, "qs")
 
         nc.gpsimd.memset(ks_pool[:].bitcast(I32)[:, 0:KS_SPLIT], 0)
-        nc.gpsimd.memset(qs[:].bitcast(I32), 0)
         nc.vector.memset(ks_pool[:].bitcast(I32)[:, KS_SPLIT : T // 4], 0)
-        nc.vector.memset(one[:], 1.0)
-        nc.scalar.activation(share[:], one[:], ACT.Identity, scale=1.0 / P)
+        nc.vector.memset(one[:, 0:1], 1.0)
+        nc.scalar.activation(share[:], one[:, 0:1], ACT.Identity, scale=1.0 / P)
         nc.vector.memset(kb_pool[0:BIAS_ROW, :], 0.0)
-        nc.vector.memset(vs_pool[0:BIAS_ROW, :], 0.0)
+        nc.gpsimd.memset(qs[:].bitcast(I32), 0)
+        nc.vector.memset(vs_pool[0:BIAS_ROW, 0:VS_SPLIT], 0.0)
+        nc.gpsimd.memset(vs_pool[0:BIAS_ROW, VS_SPLIT:T], 0.0)
 
         key_words = k_words[0].rearrange("p t r -> p (t r)").bitcast(I32)
 
@@ -136,13 +138,14 @@ def tile_attend_pkv8q_rel2_cap_kb_kernel(
             gather_scales(0, sb([P, PAGE], U8, "ks_row0")[:]),
             gather_scales(1, at(KEYS_AT, [P, 8192], U8, "ks_row1")[:, 0:PAGE]),
         ]
-        ks = [deal_scales(e, row) for e, row in enumerate(rows)]
+        rows.append(gather_scales(2, sb([P, PAGE], U8, "ks_row2")[:]))
+        ks = [deal_scales(e, rows[e]) for e in range(PAGES - 1)]
         ident = at(KEYS_AT + 6144, [P, P], F32, "ident")
         make_identity(nc, ident[:])
 
         halves = [slice(h, h + HALF) for h in range(0, PACK, HALF)]
         capped = []
-        p_t = [sb([P, PACK, NQ], F32, "p%d" % e) for e in range(PAGES - 1)]
+        p_t = [sb([P, PACK, NQ], F32, "p%d" % e) for e in range(PAGES)]
 
         def square_on_scalar(e, pos):
             for h in halves:
@@ -152,11 +155,9 @@ def tile_attend_pkv8q_rel2_cap_kb_kernel(
 
         for e in range(PAGES):
             if e == PAGES - 1:
-                row = gather_scales(e, at(KEYS_AT, [P, PAGE], U8, "ks_row2")[:])
-            kw = at(KEYS_AT + (0, 4096, 512)[e], [P, PACK, P], U32, "kw%d" % e)
+                ks.append(deal_scales(e, rows[e]))
+            kw = at(KEYS_AT + 2048 * e, [P, PACK, P], U32, "kw%d" % e)
             nc.vector.tensor_copy(kw[:].rearrange("p t s -> p s t"), kw_pool[:].bitcast(U32).indirect(page_list(e)))
-            if e == PAGES - 1:
-                ks.append(deal_scales(e, row))
             scores = [psum.tile([P, HALF, NQ], F32, name="scores%d_%d" % (e, h)) for h in range(PACK // HALF)]
             for t in range(PACK):
                 nc.tensor.matmul_mx(
@@ -169,18 +170,19 @@ def tile_attend_pkv8q_rel2_cap_kb_kernel(
                     capped[e][:, t, :], scores[t // HALF][:, t % HALF, :], ACT.Tanh,
                     scale=1.0 / CAP, bias=kb_col[e][:, t : t + 1],
                 )
-            if e == 0:
+            if e == 1:
                 square_on_scalar(0, sb([P, PACK, NQ], F32, "pos0"))
-        square_on_scalar(1, at(KEYS_AT + 512, [P, PACK, NQ], F32, "pos1"))
+        square_on_scalar(2, at(POS_AT, [P, PACK, NQ], F32, "pos2"))
 
-        vw = at(KEYS_AT + 4096, [P, PAGES * DV], U32, "vw")
+        vw = at(KEYS_AT, [P, PAGES * DV], U32, "vw")
         nc.vector.tensor_copy(vw[:], vw_pool[:].bitcast(U32).indirect(value_list[:]))
-        vsc = at(KEYS_AT + 4096 + 1536, [P, PAGES * DV], U8, "vsc")
+        nc.vector.scalar_tensor_tensor(p_t[1][:], capped[1][:], 0.0, capped[1][:], ALU.max, ALU.mult)
+        vsc = at(KEYS_AT + 1536, [P, PAGES * DV], U8, "vsc")
         nc.vector.tensor_copy(vsc[:], vsc_pool[:].indirect(value_list[:]))
 
+        order = (1, 0, 2)
         w = [sb([P, NQ * PACK], BF16, "w%d" % e) for e in range(PAGES)]
-
-        def weights(e):
+        for e in order:
             nc.vector.tensor_tensor(
                 w[e][:].rearrange("s (c i t) -> s c t i", i=PAIR, t=PACK),
                 p_t[e][:].rearrange("s t (c i) -> s c t i", i=PAIR),
@@ -188,13 +190,6 @@ def tile_attend_pkv8q_rel2_cap_kb_kernel(
                 ALU.mult,
             )
 
-        weights(0)
-        p_t.append(at(KB_AT + 4096, [P, PACK, NQ], F32, "p2"))
-        nc.vector.scalar_tensor_tensor(p_t[2][:], capped[2][:], 0.0, capped[2][:], ALU.max, ALU.mult)
-        weights(2)
-        weights(1)
-
-        order = (0, 2, 1)
         total = psum.tile([P, P], F32, name="total", tag="scores1_1")
         acc = psum.tile([P, DV], F32, name="acc")
         for e in order:
@@ -207,7 +202,7 @@ def tile_attend_pkv8q_rel2_cap_kb_kernel(
         denom = sb([P, 1], F32, "denom")
         nc.scalar.activation(parts[:], total[:], ACT.Identity, scale=CAP * CAP, bias=share[:], accum_out=denom[:])
         for e in order:
-            w_codes = at({0: 45056, 2: KEYS_AT + 512, 1: 49152}[e], [P, NQ], U32, "w_codes%d" % e)
+            w_codes = at(POS_AT + 512 * e, [P, NQ], U32, "w_codes%d" % e)
             w_scales = sb([P, NQ], U8, "w_scales%d" % e)
             nc.vector.quantize_mx(w_codes[:].bitcast(FP8X4), w_scales[:], w[e][:])
             cols = slice(e * DV, (e + 1) * DV)
@@ -217,7 +212,7 @@ def tile_attend_pkv8q_rel2_cap_kb_kernel(
                 start=(e == order[0]), stop=(e == order[-1]),
             )
 
-        inv = sb([P, 1], F32, "inv", "p1")
+        inv = sb([P, 1], F32, "inv", "p2")
         nc.vector.reciprocal(inv[:], denom[:])
         y = sb([P, DV], F32, "y")
         nc.scalar.activation(y[:], acc[:], ACT.Copy, scale=inv[:])

@@ -18,7 +18,7 @@ PAIR = 2
 
 
 KS_SPLIT = 304
-VS_SPLIT = 3000
+VS_SPLIT = 2200
 KW_CUTS = (0, 832, 2688, T)
 
 FLOPS = 2 * NQ * N * D + 2 * NQ * N * DV
@@ -134,12 +134,9 @@ def tile_attend_pkv8q_rel2_cap_kb_kernel(
             nc.vector.tensor_copy(dealt[:], row.rearrange("p (s t) -> p t s", t=PACK))
             return dealt
 
-        rows = [
-            gather_scales(0, sb([P, PAGE], U8, "ks_row0")[:]),
-            gather_scales(1, at(KEYS_AT, [P, 8192], U8, "ks_row1")[:, 0:PAGE]),
-        ]
-        rows.append(gather_scales(2, sb([P, PAGE], U8, "ks_row2")[:]))
-        ks = [deal_scales(e, rows[e]) for e in range(PAGES - 1)]
+        rows = [gather_scales(e, sb([P, PAGE], U8, "ks_row%d" % e)[:]) for e in range(PAGES - 1)]
+        rows.append(gather_scales(PAGES - 1, at(KEYS_AT, [P, 8192], U8, "ks_row2")[:, 0:PAGE]))
+        ks = [deal_scales(e, row) for e, row in enumerate(rows)]
         ident = at(KEYS_AT + 6144, [P, P], F32, "ident")
         make_identity(nc, ident[:])
 
@@ -149,13 +146,9 @@ def tile_attend_pkv8q_rel2_cap_kb_kernel(
 
         def square_on_scalar(e, pos):
             for h in halves:
-                nc.scalar.activation(pos[:, h, :], capped[e][:, h, :], ACT.Relu)
-            for h in halves:
                 nc.scalar.activation(p_t[e][:, h, :], pos[:, h, :], ACT.Square)
 
         for e in range(PAGES):
-            if e == PAGES - 1:
-                ks.append(deal_scales(e, rows[e]))
             kw = at(KEYS_AT + 2048 * e, [P, PACK, P], U32, "kw%d" % e)
             nc.vector.tensor_copy(kw[:].rearrange("p t s -> p s t"), kw_pool[:].bitcast(U32).indirect(page_list(e)))
             scores = [psum.tile([P, HALF, NQ], F32, name="scores%d_%d" % (e, h)) for h in range(PACK // HALF)]
@@ -170,9 +163,16 @@ def tile_attend_pkv8q_rel2_cap_kb_kernel(
                     capped[e][:, t, :], scores[t // HALF][:, t % HALF, :], ACT.Tanh,
                     scale=1.0 / CAP, bias=kb_col[e][:, t : t + 1],
                 )
+            if e == 0:
+                pos0 = sb([P, PACK, NQ], F32, "pos0")
+                for h in halves:
+                    nc.gpsimd.tensor_scalar(pos0[:, h, :], capped[0][:, h, :], CAP, 0.0, ALU.min, ALU.max)
             if e == 1:
-                square_on_scalar(0, sb([P, PACK, NQ], F32, "pos0"))
-        square_on_scalar(2, at(POS_AT, [P, PACK, NQ], F32, "pos2"))
+                square_on_scalar(0, pos0)
+        pos2 = at(POS_AT, [P, PACK, NQ], F32, "pos2")
+        for h in halves:
+            nc.scalar.activation(pos2[:, h, :], capped[2][:, h, :], ACT.Relu)
+        square_on_scalar(2, pos2)
 
         vw = at(KEYS_AT, [P, PAGES * DV], U32, "vw")
         nc.vector.tensor_copy(vw[:], vw_pool[:].bitcast(U32).indirect(value_list[:]))
@@ -180,7 +180,7 @@ def tile_attend_pkv8q_rel2_cap_kb_kernel(
         vsc = at(KEYS_AT + 1536, [P, PAGES * DV], U8, "vsc")
         nc.vector.tensor_copy(vsc[:], vsc_pool[:].indirect(value_list[:]))
 
-        order = (1, 0, 2)
+        order = (0, 1, 2)
         w = [sb([P, NQ * PACK], BF16, "w%d" % e) for e in range(PAGES)]
         for e in order:
             nc.vector.tensor_tensor(

@@ -70,7 +70,7 @@ def tile_attend_pkv8q_rel2_cap_kb_kernel(
         nc.gpsimd.memset(ks_pool[:].bitcast(I32)[:, 0:KS_SPLIT], 0)
         nc.vector.memset(ks_pool[:].bitcast(I32)[:, KS_SPLIT : T // 4], 0)
         nc.vector.memset(one[:, 0:1], 1.0)
-        nc.scalar.activation(share[:], one[:, 0:1], ACT.Identity, scale=1.0 / P)
+        nc.scalar.activation(share[:], one[:, 0:1], ACT.Identity, scale=1.0 / (P * CAP * CAP))
         nc.vector.memset(kb_pool[0:BIAS_ROW, :], 0.0)
         nc.gpsimd.memset(qs[:].bitcast(I32), 0)
         nc.vector.memset(vs_pool[0:BIAS_ROW, 0:VS_SPLIT], 0.0)
@@ -99,17 +99,20 @@ def tile_attend_pkv8q_rel2_cap_kb_kernel(
             cols = PAGE // LIST_ROWS
             return key_list[:, e * cols : (e + 1) * cols]
 
-        def columns(name, pool, factor, base):
+        def columns(name, pool, factor, base, on_scalar):
             cols = []
             for e in range(PAGES):
                 row = sb([P, PAGE], F32, "%s_row%d" % (name, e))
-                nc.scalar.activation(row[:], pool[:].indirect(page_list(e)), ACT.Copy, scale=factor)
+                if e < on_scalar:
+                    nc.scalar.activation(row[:], pool[:].indirect(page_list(e)), ACT.Copy, scale=factor)
+                else:
+                    nc.vector.tensor_copy(row[:], pool[:].indirect(page_list(e)))
                 col = at(base + 1024 * e, [P, PACK], F32, "%s_col%d" % (name, e))
                 nc.sync.dma_start(col[:], row[BIAS_ROW:P, :])
                 cols.append(col)
             return cols
 
-        kb_col = columns("kb", kb_pool, 1.0 / CAP, 45056 - 2048)
+        kb_col = columns("kb", kb_pool, 1.0 / CAP, 45056 - 2048, PAGES)
 
         vw_pool = at(KB_AT + 8192, [P, POOL_PAGES * DV], I32, "vw_pool")
         nc.sync.dma_start(
@@ -123,8 +126,6 @@ def tile_attend_pkv8q_rel2_cap_kb_kernel(
                 scale_rows(vsc_pool, g).rearrange("p (u e) -> p u e", u=POOL_PAGES),
                 v_scales.rearrange("u (a r) e -> r a u e", r=4)[g].bitcast(I32),
             )
-        vs_col = columns("vs", vs_pool, CAP * CAP, COLS_AT)
-
         def gather_scales(e, row):
             nc.vector.tensor_copy(row, ks_pool[:].indirect(page_list(e)))
             return row
@@ -137,6 +138,7 @@ def tile_attend_pkv8q_rel2_cap_kb_kernel(
         rows = [gather_scales(e, sb([P, PAGE], U8, "ks_row%d" % e)[:]) for e in range(PAGES - 1)]
         rows.append(gather_scales(PAGES - 1, at(KEYS_AT, [P, 8192], U8, "ks_row2")[:, 0:PAGE]))
         ks = [deal_scales(e, row) for e, row in enumerate(rows)]
+        vs_col = columns("vs", vs_pool, 1.0, COLS_AT, PAGES - 1)
         ident = at(KEYS_AT + 6144, [P, P], F32, "ident")
         make_identity(nc, ident[:])
 
@@ -200,7 +202,7 @@ def tile_attend_pkv8q_rel2_cap_kb_kernel(
                 )
         parts = sb([P, P], F32, "parts")
         denom = sb([P, 1], F32, "denom")
-        nc.scalar.activation(parts[:], total[:], ACT.Identity, scale=CAP * CAP, bias=share[:], accum_out=denom[:])
+        nc.scalar.activation(parts[:], total[:], ACT.Identity, bias=share[:], accum_out=denom[:])
         for e in order:
             w_codes = at(POS_AT + 512 * e, [P, NQ], U32, "w_codes%d" % e)
             w_scales = sb([P, NQ], U8, "w_scales%d" % e)

from contextlib import ExitStack

import concourse.mybir as mybir
from concourse.masks import make_identity

N, T, D, DV, NQ = 1536, 4096, 512, 128, 128
PAGE = 512
PAGES = N // PAGE
POOL_PAGES = T // PAGE
CAP = 2.0
P = 128
PACK = 4
QUADRANTS = 4
LIST_ROWS = 16
BIAS_ROW = P - 1
HALF = 2
PAIR = 2


KS_SPLIT = 304
VS_SPLIT = 2200
KW_CUTS = (0, 832, 2688, T)

FLOPS = 2 * NQ * N * D + 2 * NQ * N * DV
BYTES = (T * D + T * DV + NQ * D) * 33 // 32 + 2 * 4 * T + 2 * P * (N + PAGES * DV) // LIST_ROWS + 4 * NQ * DV

F32 = mybir.dt.float32
BF16 = mybir.dt.bfloat16
I32 = mybir.dt.int32
U32 = mybir.dt.uint32
U16 = mybir.dt.uint16
U8 = mybir.dt.uint8
FP8X4 = mybir.dt.float8_e4m3fn_x4
ALU = mybir.AluOpType
ACT = mybir.ActivationFunctionType


def tile_attend_pkv8q_rel2_cap_kb_kernel(
    tc, q_words, q_scales, k_words, k_scales, v_words, v_scales, vs, kb, offs, voffs, out
):
    nc = tc.nc
    with ExitStack() as ctx:
        lists = ctx.enter_context(tc.tile_pool(name="lists", bufs=1))
        held = ctx.enter_context(tc.tile_pool(name="held", bufs=1))
        placed = ctx.enter_context(tc.tile_pool(name="placed", bufs=1))
        psum = ctx.enter_context(tc.psum_pool(name="psum", bufs=1))

        def sb(shape, dtype, name, tag=None):
            return held.tile(shape, dtype, name=name, tag=tag or name, align_bytes=64)

        def at(offset, shape, dtype, name):
            return placed.tile(shape, dtype, name=name, align_bytes=64, offset=offset)

        def scale_rows(plane, r):
            return plane[r:P:32, :].bitcast(I32)

        KB_AT, COLS_AT, POS_AT, KEYS_AT, VS_AT, Q_AT, KW_AT = 0, 16384, 20480, 32768, 49152, 65536, 81920

        key_list = lists.tile([P, N // LIST_ROWS], U16, name="key_list")
        value_list = lists.tile([P, PAGES * DV // LIST_ROWS], U16, name="value_list")
        one = at(Q_AT - 64, [P, 32], F32, "one")
        share = sb([P, 1], F32, "share")
        kw_pool = at(KW_AT, [P, T], I32, "kw_pool")
        ks_pool = sb([P, T], U8, "ks_pool")
        kb_pool = at(KB_AT, [P, T], F32, "kb_pool")
        vs_pool = at(VS_AT, [P, T], F32, "vs_pool")
        qw = sb([P, NQ], I32, "qw")
        qs = at(Q_AT, [P, NQ], U8, "qs")

        nc.gpsimd.memset(ks_pool[:].bitcast(I32)[:, 0:KS_SPLIT], 0)
        nc.vector.memset(ks_pool[:].bitcast(I32)[:, KS_SPLIT : T // 4], 0)
        nc.vector.memset(one[:, 0:1], 1.0)
        nc.scalar.activation(share[:], one[:, 0:1], ACT.Identity, scale=1.0 / (P * CAP * CAP))
        nc.vector.memset(kb_pool[0:BIAS_ROW, :], 0.0)
        nc.gpsimd.memset(qs[:].bitcast(I32), 0)
        nc.vector.memset(vs_pool[0:BIAS_ROW, 0:VS_SPLIT], 0.0)
        nc.gpsimd.memset(vs_pool[0:BIAS_ROW, VS_SPLIT:T], 0.0)

        key_words = k_words[0].rearrange("p t r -> p (t r)").bitcast(I32)

        def load_keys(i):
            part = slice(KW_CUTS[i], KW_CUTS[i + 1])
            nc.sync.dma_start(kw_pool[:, part], key_words[:, part])

        nc.sync.dma_start(key_list[:], offs)
        nc.sync.dma_start(kb_pool[BIAS_ROW:P, :], kb[0:1, :])
        nc.sync.dma_start(value_list[:], voffs)
        load_keys(0)
        for g in range(QUADRANTS):
            nc.sync.dma_start(scale_rows(ks_pool, g), k_scales[0].rearrange("(a r) t -> r a t", r=4)[g].bitcast(I32))
        nc.sync.dma_start(vs_pool[BIAS_ROW:P, :], vs[0:1, :])
        load_keys(1)
        nc.sync.dma_start(qw[:], q_words[0, 0].rearrange("p q r -> p (q r)").bitcast(I32))
        for g in range(QUADRANTS):
            nc.sync.dma_start(scale_rows(qs, g), q_scales[0, 0].rearrange("(a r) q -> r a q", r=4)[g].bitcast(I32))
        load_keys(2)

        def page_list(e):
            cols = PAGE // LIST_ROWS
            return key_list[:, e * cols : (e + 1) * cols]

        def columns(name, pool, factor, base, on_scalar):
            cols = []
            for e in range(PAGES):
                row = sb([P, PAGE], F32, "%s_row%d" % (name, e))
                if e < on_scalar:
                    nc.scalar.activation(row[:], pool[:].indirect(page_list(e)), ACT.Copy, scale=factor)
                else:
                    nc.vector.tensor_copy(row[:], pool[:].indirect(page_list(e)))
                col = at(base + 1024 * e, [P, PACK], F32, "%s_col%d" % (name, e))
                nc.sync.dma_start(col[:], row[BIAS_ROW:P, :])
                cols.append(col)
            return cols

        kb_col = columns("kb", kb_pool, 1.0 / CAP, 45056 - 2048, PAGES)

        vw_pool = at(KB_AT + 8192, [P, POOL_PAGES * DV], I32, "vw_pool")
        nc.sync.dma_start(
            vw_pool[:].rearrange("p (u e) -> p u e", u=POOL_PAGES),
            v_words.rearrange("u p e r -> p u (e r)").bitcast(I32),
        )
        vsc_pool = at(KB_AT + 4096, [P, POOL_PAGES * DV], U8, "vsc_pool")
        nc.gpsimd.memset(vsc_pool[:].bitcast(I32), 0)
        for g in range(QUADRANTS):
            nc.sync.dma_start(
                scale_rows(vsc_pool, g).rearrange("p (u e) -> p u e", u=POOL_PAGES),
                v_scales.rearrange("u (a r) e -> r a u e", r=4)[g].bitcast(I32),
            )
        def gather_scales(e, row):
            nc.vector.tensor_copy(row, ks_pool[:].indirect(page_list(e)))
            return row

        def deal_scales(e, row):
            dealt = sb([P, PACK, P], U8, "ks%d" % e)
            nc.vector.tensor_copy(dealt[:], row.rearrange("p (s t) -> p t s", t=PACK))
            return dealt

        rows = [gather_scales(e, sb([P, PAGE], U8, "ks_row%d" % e)[:]) for e in range(PAGES - 1)]
        rows.append(gather_scales(PAGES - 1, at(KEYS_AT, [P, 8192], U8, "ks_row2")[:, 0:PAGE]))
        ks = [deal_scales(e, row) for e, row in enumerate(rows)]
        vs_col = columns("vs", vs_pool, 1.0, COLS_AT, PAGES - 1)
        ident = at(KEYS_AT + 6144, [P, P], F32, "ident")
        make_identity(nc, ident[:])

        halves = [slice(h, h + HALF) for h in range(0, PACK, HALF)]
        capped = []
        p_t = [sb([P, PACK, NQ], F32, "p%d" % e) for e in range(PAGES)]

        def square_on_scalar(e, pos):
            for h in halves:
                nc.scalar.activation(p_t[e][:, h, :], pos[:, h, :], ACT.Square)

        for e in range(PAGES):
            kw = at(KEYS_AT + 2048 * e, [P, PACK, P], U32, "kw%d" % e)
            nc.vector.tensor_copy(kw[:].rearrange("p t s -> p s t"), kw_pool[:].bitcast(U32).indirect(page_list(e)))
            scores = [psum.tile([P, HALF, NQ], F32, name="scores%d_%d" % (e, h)) for h in range(PACK // HALF)]
            for t in range(PACK):
                nc.tensor.matmul_mx(
                    scores[t // HALF][:, t % HALF, :], lhsT=kw[:, t, :].bitcast(FP8X4), lhsT_scale=ks[e][:, t, :],
                    rhs=qw[:].bitcast(FP8X4), rhs_scale=qs[:], start=True, stop=True,
                )
            capped.append(at(VS_AT + 2048 * e, [P, PACK, NQ], F32, "capped%d" % e))
            for t in range(PACK):
                nc.scalar.activation(
                    capped[e][:, t, :], scores[t // HALF][:, t % HALF, :], ACT.Tanh,
                    scale=1.0 / CAP, bias=kb_col[e][:, t : t + 1],
                )
            if e == 0:
                pos0 = sb([P, PACK, NQ], F32, "pos0")
                for h in halves:
                    nc.gpsimd.tensor_scalar(pos0[:, h, :], capped[0][:, h, :], CAP, 0.0, ALU.min, ALU.max)
            if e == 1:
                square_on_scalar(0, pos0)
        pos2 = at(POS_AT, [P, PACK, NQ], F32, "pos2")
        for h in halves:
            nc.scalar.activation(pos2[:, h, :], capped[2][:, h, :], ACT.Relu)
        square_on_scalar(2, pos2)

        vw = at(KEYS_AT, [P, PAGES * DV], U32, "vw")
        nc.vector.tensor_copy(vw[:], vw_pool[:].bitcast(U32).indirect(value_list[:]))
        nc.vector.scalar_tensor_tensor(p_t[1][:], capped[1][:], 0.0, capped[1][:], ALU.max, ALU.mult)
        vsc = at(KEYS_AT + 1536, [P, PAGES * DV], U8, "vsc")
        nc.vector.tensor_copy(vsc[:], vsc_pool[:].indirect(value_list[:]))

        order = (0, 1, 2)
        w = [sb([P, NQ * PACK], BF16, "w%d" % e) for e in range(PAGES)]
        for e in order:
            nc.vector.tensor_tensor(
                w[e][:].rearrange("s (c i t) -> s c t i", i=PAIR, t=PACK),
                p_t[e][:].rearrange("s t (c i) -> s c t i", i=PAIR),
                vs_col[e][:].unsqueeze(1).unsqueeze(3).to_broadcast([P, NQ // PAIR, PACK, PAIR]),
                ALU.mult,
            )

        total = psum.tile([P, P], F32, name="total", tag="scores1_1")
        acc = psum.tile([P, DV], F32, name="acc")
        for e in order:
            for t in range(PACK):
                nc.tensor.matmul(
                    total[:], lhsT=p_t[e][:, t, :], rhs=ident[:], is_transpose=True,
                    start=(e == order[0] and t == 0), stop=(e == order[-1] and t == PACK - 1),
                )
        parts = sb([P, P], F32, "parts")
        denom = sb([P, 1], F32, "denom")
        nc.scalar.activation(parts[:], total[:], ACT.Identity, bias=share[:], accum_out=denom[:])
        for e in order:
            w_codes = at(POS_AT + 512 * e, [P, NQ], U32, "w_codes%d" % e)
            w_scales = sb([P, NQ], U8, "w_scales%d" % e)
            nc.vector.quantize_mx(w_codes[:].bitcast(FP8X4), w_scales[:], w[e][:])
            cols = slice(e * DV, (e + 1) * DV)
            nc.tensor.matmul_mx(
                acc[:], lhsT=w_codes[:].bitcast(FP8X4), lhsT_scale=w_scales[:],
                rhs=vw[:, cols].bitcast(FP8X4), rhs_scale=vsc[:, cols],
                start=(e == order[0]), stop=(e == order[-1]),
            )

        inv = sb([P, 1], F32, "inv", "p2")
        nc.vector.reciprocal(inv[:], denom[:])
        y = sb([P, DV], F32, "y")
        nc.scalar.activation(y[:], acc[:], ACT.Copy, scale=inv[:])
        nc.sync.dma_start(out[0], y[:])
